import numpy as np
import ml_dtypes


def mxq(x, axis, fmt="e4m3"):
    dtype, down = {"e4m3": (ml_dtypes.float8_e4m3fn, 7), "e5m2": (ml_dtypes.float8_e5m2, 14)}[fmt]
    v = np.moveaxis(np.asarray(x, np.float32).astype(ml_dtypes.bfloat16).astype(np.float64), axis, -1)
    blocks = v.reshape(v.shape[:-1] + (-1, 32))
    amax = np.abs(blocks).max(-1, keepdims=True)
    byte = np.maximum(np.where(amax > 0, np.frexp(amax)[1] - 1 + 127, 0) - down, 1)
    scale = np.exp2(byte - 127.0)
    codes = (blocks / scale).astype(np.float32).astype(dtype).astype(np.float64)
    return np.moveaxis((codes * scale).reshape(v.shape), -1, axis)


WIDE = False


def mx_kscale(k):
    if not WIDE:
        return np.ones(k)
    levels = np.array([24, -24, 12, -12, 0])
    if k % 512:
        return np.exp2(np.random.permutation(np.resize(levels, k // 32))).repeat(32)
    a = np.empty((k // 512, 16))
    for p in range(k // 512):
        a[p, :8] = np.random.permutation(np.resize(levels, 8))
        for g in range(8):
            far = levels[np.abs(levels - a[p, g]) >= 10]
            a[p, g + 8] = far[np.random.randint(len(far))]
    return np.exp2(a.ravel()).repeat(32)


def f64(x):
    return np.asarray(x).astype(np.float64)


def striped(idx):
    return np.tile(idx.reshape(-1, 16).T, (8, 1)).astype(np.uint16)


def unstriped(offs):
    return offs[:16].T.reshape(-1).astype(np.int64)


E2M1 = np.array([0.0, 0.5, 1.0, 1.5, 2.0, 3.0, 4.0, 6.0, -0.0, -0.5, -1.0, -1.5, -2.0, -3.0, -4.0, -6.0])


def pack_weight(w, fmt):
    k, n = w.shape
    w = f64(np.asarray(w, np.float32).astype(ml_dtypes.bfloat16)).reshape(k // 32, 32, n)
    amax = np.abs(w).max(1)
    if fmt == "e4m3":
        byte = np.frexp(amax)[1] - 1 + 127 - 7
    else:
        mant, ex = np.frexp(amax / 6.0)
        byte = np.where(mant > 0.5, ex, ex - 1) + 127
    byte = np.clip(np.where(amax > 0, byte, 1), 1, 254)
    scaled = (w * np.exp2(127.0 - byte)[:, None, :]).reshape(k, n).astype(np.float32)
    by_word = np.ascontiguousarray(scaled.reshape(k // 512, 128, 4, n).transpose(0, 1, 3, 2))
    if fmt == "e4m3":
        words = by_word.astype(ml_dtypes.float8_e4m3fn).view(np.uint8)
    else:
        c = by_word.astype(ml_dtypes.float4_e2m1fn).view(np.uint8) & 0xF
        words = (c[..., 0::2] | (c[..., 1::2] << 4)).reshape(k // 512, 128, 2 * n)
    return np.ascontiguousarray(words), np.ascontiguousarray(byte.astype(np.uint8).reshape(k // 512, 16, n))


def unpack_weight(words, scales, fmt):
    g, _, n = scales.shape
    words = np.ascontiguousarray(words).reshape(g, 128, n, -1)
    if fmt == "e4m3":
        vals = words.view(ml_dtypes.float8_e4m3fn).astype(np.float64)
    else:
        nib = np.empty((g, 128, n, 4), np.uint8)
        nib[..., 0::2] = words & 0xF
        nib[..., 1::2] = words >> 4
        vals = E2M1[nib]
    vals = vals * np.repeat(np.exp2(scales.astype(np.float64) - 127.0), 8, axis=1)[..., None]
    return vals.transpose(0, 1, 3, 2).reshape(g * 512, n)


K, R, N, T, J = 512, 512, 512, 1024, 512


def setup_inputs():
    n = np.random.standard_normal
    s = mx_kscale(K)[:, None]
    u = mx_kscale(R)[:, None]
    wb = 0.7 * n((K, N)) / np.sqrt(K) / s
    wb4 = pack_weight(wb, "e2m1")
    wbrest = wb - unpack_weight(*wb4, "e2m1")
    p_tab = pack_weight(n((K, T)) * s, "e4m3")
    p_wb8 = pack_weight(wbrest, "e4m3")
    p_dn = pack_weight(n((K, R)) / np.sqrt(K) / s * u.T, "e2m1")
    return {
        "tab_words": p_tab[0],
        "tab_scales": p_tab[1],
        "wb4_words": wb4[0],
        "wb4_scales": wb4[1],
        "wb8_words": p_wb8[0],
        "wb8_scales": p_wb8[1],
        "dn_words": p_dn[0],
        "dn_scales": p_dn[1],
        "upw": (2.0 * n((R, N)) / np.sqrt(R) / u).astype(np.float32),
        "x0T": (n((N, T))).astype(np.float32),
        "b": (0.3 * n(N)).astype(np.float32),
        "offs": striped(np.random.permutation(T)[:J]),
    }


def reference(tab_words, tab_scales, wb4_words, wb4_scales, wb8_words, wb8_scales, dn_words, dn_scales, upw, x0T, b, offs):
    idx = unstriped(offs)
    tab_ = unpack_weight(tab_words, tab_scales, "e4m3")[:, idx]
    wb4_ = unpack_weight(wb4_words, wb4_scales, "e2m1")
    wb8_ = unpack_weight(wb8_words, wb8_scales, "e4m3")
    dn_ = unpack_weight(dn_words, dn_scales, "e2m1")
    hs = dn_.T @ tab_
    h = np.maximum(hs, 0.0)
    h_ = mxq(h, 0, "e4m3")
    upw_ = mxq(f64(upw), 0, "e4m3")
    y = wb4_.T @ tab_ + wb8_.T @ tab_ + upw_.T @ h_
    return f64(x0T)[:, idx] * (y + f64(b)[:, None]) + f64(x0T)[:, idx]

@@ -1,0 +1,250 @@
+from contextlib import ExitStack
+
+import concourse.mybir as mybir
+
+K, R, N, T, J = 512, 512, 512, 1024, 512
+FLOPS = 2 * J * (K * R + 2 * K * N + R * N)
+
+F32 = mybir.dt.float32
+BF16 = mybir.dt.bfloat16
+I32 = mybir.dt.int32
+U32 = mybir.dt.uint32
+U16 = mybir.dt.uint16
+U8 = mybir.dt.uint8
+FP8X4 = mybir.dt.float8_e4m3fn_x4
+FP4X4 = mybir.dt.float4_e2m1fn_x4
+ACT = mybir.ActivationFunctionType
+ALU = mybir.AluOpType
+
+P = 128
+PACK = 4
+LIST_ROWS = 16
+
+
+def tile_list_xcross_res_relu_kernel(
+    tc, tab_words, tab_scales, wb4_words, wb4_scales, wb8_words, wb8_scales, dn_words, dn_scales, upw, x0T, b, offs, out
+):
+    nc = tc.nc
+    with ExitStack() as ctx:
+        keep = ctx.enter_context(tc.tile_pool(name="keep", bufs=1))
+        psum = ctx.enter_context(tc.psum_pool(name="psum", bufs=1))
+
+        offsets = keep.tile([P, J // LIST_ROWS], U16, name="offsets")
+        tab_w = keep.tile([P, T], I32, name="tab_w", align_bytes=64)
+        tab_s = keep.tile([P, T // 4], I32, name="tab_s", align_bytes=64)
+        dn_w = keep.tile([P, R // 2], I32, name="dn_w", align_bytes=64)
+        dn_s = keep.tile([P, R // 4], I32, name="dn_s", align_bytes=64)
+        wb4_w = keep.tile([P, N // 2], I32, name="wb4_w", align_bytes=64)
+        wb4_s = keep.tile([P, N // 4], I32, name="wb4_s", align_bytes=64)
+        wb8_w = keep.tile([P, N], I32, name="wb8_w", align_bytes=64)
+        wb8_s = keep.tile([P, N // 4], I32, name="wb8_s", align_bytes=64)
+        up_raw = [keep.tile([P, PACK, N // 2], F32, name="up_raw%d" % u) for u in range(2)]
+        x0 = [keep.tile([P, T], F32, name="x0_%d" % i) for i in range(4)]
+        b_col = keep.tile([P, 4], F32, name="b_col")
+        b_plus = keep.tile([P, 4], F32, name="b_plus")
+        up_view = upw.rearrange("(p i) n -> p i n", i=PACK)
+
+        def load_scales(queue, plane, src):
+            rows = src[0].bitcast(I32)
+            for q in range(4):
+                queue.dma_start(out=plane[32 * q : 32 * q + 4, :], in_=rows[4 * q : 4 * q + 4, :])
+
+        warm_in = keep.tile([P, 1], F32, name="warm_in")
+        warm_out = keep.tile([P, 1], F32, name="warm_out")
+        nc.vector.memset(tab_s[:], 0)
+        nc.vector.memset(warm_in[:], 0.0)
+        nc.vector.memset(dn_s[:], 0)
+        nc.scalar.activation(out=warm_out[:], in_=warm_in[:], func=ACT.Copy, bias=1.0)
+        nc.sync.dma_start(offsets[:], offs)
+        load_scales(nc.sync, tab_s, tab_scales)
+        nc.sync.dma_start(out=dn_w[:], in_=dn_words[0].bitcast(I32))
+        nc.sync.dma_start(out=tab_w[:], in_=tab_words[0].rearrange("p t i -> p (t i)").bitcast(I32))
+        nc.sync.dma_start(out=up_raw[0][:], in_=up_view[:, :, 0 : 256])
+        load_scales(nc.sync, dn_s, dn_scales)
+        nc.sync.dma_start(out=up_raw[1][:], in_=up_view[:, :, 256 : 512])
+        nc.sync.dma_start(out=wb8_w[:], in_=wb8_words[0].rearrange("p n i -> p (n i)").bitcast(I32))
+        nc.sync.dma_start(out=wb4_w[:], in_=wb4_words[0].bitcast(I32))
+        load_scales(nc.sync, wb4_s, wb4_scales)
+        nc.sync.dma_start(out=x0[0][:], in_=x0T[0 * P : 1 * P, :])
+        nc.sync.dma_start(out=x0[1][:], in_=x0T[1 * P : 2 * P, :])
+        nc.sync.dma_start(out=x0[2][:], in_=x0T[2 * P : 3 * P, :])
+        nc.sync.dma_start(out=x0[3][:], in_=x0T[3 * P : 4 * P, :])
+        load_scales(nc.gpsimd, wb8_s, wb8_scales)
+        with nc.allow_non_contiguous_dma(reason="one bias value to a partition"):
+            nc.gpsimd.dma_start(out=b_col[:], in_=b.rearrange("(i p) -> p i", p=P))
+
+        nc.gpsimd.tensor_scalar(out=b_plus[:], in0=b_col[:], scalar1=1.0, scalar2=warm_out[:], op0=ALU.mult, op1=ALU.add)
+
+        dn_wp = keep.tile([P, 2 * R], U8, name="dn_wp", align_bytes=64)
+        dn_sp = keep.tile([P, R], U8, name="dn_sp", align_bytes=64)
+        v_w = keep.tile([P, J], U32, name="v_w", align_bytes=64)
+        v_s = keep.tile([P, J], U8, name="v_s", align_bytes=64)
+        up_b = keep.tile([P, N * PACK], BF16, name="up_b", align_bytes=64)
+        up_w = keep.tile([P, N], U32, name="up_w", align_bytes=64)
+        up_s = keep.tile([P, N], U8, name="up_s", align_bytes=64)
+        h_b = keep.tile([P, J * PACK], BF16, name="h_b", align_bytes=64)
+        h_w = keep.tile([P, J], U32, name="h_w", align_bytes=64)
+        h_s = keep.tile([P, J], U8, name="h_s", align_bytes=64)
+        h_ps = [psum.tile([P, PACK, P], F32, name="h_ps%d" % c) for c in range(4)]
+        y_ps = [psum.tile([P, J], F32, name="y_ps%d" % i) for i in range(4)]
+        y_sb = [keep.tile([P, J], F32, name="y_sb%d" % i) for i in range(4)]
+        res = [keep.tile([P, J], F32, name="res%d" % i) for i in range(4)]
+
+        def listed(lo, hi):
+            return offsets[:, lo // LIST_ROWS : hi // LIST_ROWS]
+
+        def gather_s(lo, hi):
+            nc.vector.tensor_copy(out=v_s[:, lo:hi], in_=tab_s[:].bitcast(U8).indirect(listed(lo, hi)))
+
+        def gather_w(lo, hi):
+            nc.vector.tensor_copy(out=v_w[:, lo:hi], in_=tab_w[:].bitcast(U32).indirect(listed(lo, hi)))
+
+        def perm_w():
+            nc.vector.tensor_copy(
+                out=dn_wp[:].bitcast(U16).rearrange("p (t m) -> p t m", t=PACK),
+                in_=dn_w[:].bitcast(U16).rearrange("p (m t) -> p t m", t=PACK),
+            )
+
+        def perm_s():
+            nc.vector.tensor_copy(
+                out=dn_sp[:].rearrange("p (t m) -> p t m", t=PACK),
+                in_=dn_s[:].bitcast(U8).rearrange("p (m t) -> p t m", t=PACK),
+            )
+
+        def h_mm(c):
+            cols = slice(c * P, (c + 1) * P)
+            for t in range(PACK):
+                nc.tensor.matmul_mx(
+                    out=h_ps[c][:, t, :],
+                    lhsT=dn_wp[:, 2 * t * P : 2 * (t + 1) * P].bitcast(FP4X4),
+                    lhsT_scale=dn_sp[:, t * P : (t + 1) * P],
+                    rhs=v_w[:, cols].bitcast(FP8X4),
+                    rhs_scale=v_s[:, cols],
+                    start=True,
+                    stop=True,
+                )
+
+        def h_relu(c):
+            nc.scalar.activation(
+                out=h_b[:, c * P * PACK : (c + 1) * P * PACK].rearrange("p (j t) -> p j t", t=PACK),
+                in_=h_ps[c][:].rearrange("p t j -> p j t"),
+                func=ACT.Relu,
+            )
+
+        def h_relu_v(c):
+            nc.vector.tensor_scalar(
+                out=h_b[:, c * P * PACK : (c + 1) * P * PACK].rearrange("p (j t) -> p j t", t=PACK),
+                in0=h_ps[c][:].rearrange("p t j -> p j t"),
+                scalar1=0.0,
+                scalar2=None,
+                op0=ALU.max,
+            )
+
+        def h_quant(lo, hi):
+            nc.vector.quantize_mx(out=h_w[:, lo:hi].bitcast(FP8X4), scales=h_s[:, lo:hi], in_=h_b[:, lo * PACK : hi * PACK])
+
+        def up_cast(u, on_vector):
+            half = N // 2
+            dst = up_b[:, u * half * PACK : (u + 1) * half * PACK].rearrange("p (c e i) -> p c i e", e=4, i=PACK)
+            src = up_raw[u][:].rearrange("p i (c e) -> p c i e", e=4)
+            if on_vector:
+                nc.vector.tensor_copy(out=dst, in_=src)
+            else:
+                nc.scalar.copy(out=dst, in_=src)
+
+        def up_quant(u):
+            half = N // 2
+            cols = slice(u * half, (u + 1) * half)
+            nc.vector.quantize_mx(
+                out=up_w[:, cols].bitcast(FP8X4), scales=up_s[:, cols], in_=up_b[:, u * half * PACK : (u + 1) * half * PACK]
+            )
+
+        def up_quant_all():
+            nc.vector.quantize_mx(out=up_w[:].bitcast(FP8X4), scales=up_s[:], in_=up_b[:])
+
+        def pre_gather(i):
+            nc.vector.tensor_copy(out=y_sb[i][:], in_=x0[i][:].indirect(offsets[:]))
+
+        def cross_psum(i):
+            nc.vector.scalar_tensor_tensor(
+                out=res[i][:], in0=y_ps[i][:], scalar=b_plus[:, i : i + 1], in1=y_sb[i][:], op0=ALU.add, op1=ALU.mult
+            )
+
+        def y_wb4(i, start, stop):
+            nc.tensor.matmul_mx(
+                out=y_ps[i][:],
+                lhsT=wb4_w[:].bitcast(U8)[:, 2 * i * P : 2 * (i + 1) * P].bitcast(FP4X4),
+                lhsT_scale=wb4_s[:].bitcast(U8)[:, i * P : (i + 1) * P],
+                rhs=v_w[:].bitcast(FP8X4),
+                rhs_scale=v_s[:],
+                start=start,
+                stop=stop,
+            )
+
+        def y_wb8(i, start, stop):
+            nc.tensor.matmul_mx(
+                out=y_ps[i][:],
+                lhsT=wb8_w[:, i * P : (i + 1) * P].bitcast(FP8X4),
+                lhsT_scale=wb8_s[:].bitcast(U8)[:, i * P : (i + 1) * P],
+                rhs=v_w[:].bitcast(FP8X4),
+                rhs_scale=v_s[:],
+                start=start,
+                stop=stop,
+            )
+
+        def y_up(i, start, stop):
+            nc.tensor.matmul_mx(
+                out=y_ps[i][:],
+                lhsT=up_w[:, i * P : (i + 1) * P].bitcast(FP8X4),
+                lhsT_scale=up_s[:, i * P : (i + 1) * P],
+                rhs=h_w[:].bitcast(FP8X4),
+                rhs_scale=h_s[:],
+                start=start,
+                stop=stop,
+            )
+
+        def y_out(i, lo, hi):
+            nc.scalar.activation(out=y_sb[i][:, lo:hi], in_=y_ps[i][:, lo:hi], func=ACT.Identity, bias=b_plus[:, i : i + 1])
+
+        def cross(i, lo, hi):
+            nc.vector.tensor_tensor(out=res[i][:, lo:hi], in0=x0[i][:].indirect(listed(lo, hi)), in1=y_sb[i][:, lo:hi], op=ALU.mult)
+
+        def store(i, lo, hi):
+            nc.sync.dma_start(out=out[i * P : (i + 1) * P, lo:hi], in_=res[i][:, lo:hi])
+
+        gather_s(0, 512)
+        perm_w()
+        gather_w(0, 512)
+        perm_s()
+        up_cast(0, False)
+        for c in range(4):
+            h_mm(c)
+        for c in range(4):
+            h_relu(c)
+        up_cast(1, True)
+        up_quant_all()
+        h_quant(0, 256)
+        h_quant(256, 384)
+        h_quant(384, 512)
+        pre_gather(0)
+        for i in (1, 0):
+            y_wb4(i, True, False)
+            y_wb8(i, False, False)
+        y_up(1, False, True)
+        y_up(0, False, True)
+        for i in (2, 3):
+            y_wb4(i, True, False)
+            y_wb8(i, False, False)
+            y_up(i, False, True)
+        y_out(1, 0, J)
+        cross_psum(0)
+        store(0, 0, J)
+        cross(1, 0, J)
+        store(1, 0, J)
+        y_out(2, 0, J)
+        cross(2, 0, J)
+        store(2, 0, J)
+        for lo in (0, 256):
+            y_out(3, lo, lo + 256)
+            cross(3, lo, lo + 256)
+            store(3, lo, lo + 256)

@@ -56,24 +56,27 @@ def tile_list_xcross_res_relu_kernel(
         nc.vector.memset(dn_s[:], 0)
         nc.scalar.activation(out=warm_out[:], in_=warm_in[:], func=ACT.Copy, bias=1.0)
         nc.sync.dma_start(offsets[:], offs)
+        nc.sync.dma_start(out=tab_w[:], in_=tab_words[0].rearrange("p t i -> p (t i)").bitcast(I32))
         load_scales(nc.sync, tab_s, tab_scales)
         nc.sync.dma_start(out=dn_w[:], in_=dn_words[0].bitcast(I32))
-        nc.sync.dma_start(out=tab_w[:], in_=tab_words[0].rearrange("p t i -> p (t i)").bitcast(I32))
         nc.sync.dma_start(out=up_raw[0][:], in_=up_view[:, :, 0 : 256])
         load_scales(nc.sync, dn_s, dn_scales)
-        nc.sync.dma_start(out=up_raw[1][:], in_=up_view[:, :, 256 : 512])
-        nc.sync.dma_start(out=wb8_w[:], in_=wb8_words[0].rearrange("p n i -> p (n i)").bitcast(I32))
         nc.sync.dma_start(out=wb4_w[:], in_=wb4_words[0].bitcast(I32))
+        nc.sync.dma_start(out=up_raw[1][:], in_=up_view[:, :, 256 : 512])
         load_scales(nc.sync, wb4_s, wb4_scales)
         nc.sync.dma_start(out=x0[0][:], in_=x0T[0 * P : 1 * P, :])
+        nc.sync.dma_start(out=wb8_w[:], in_=wb8_words[0].rearrange("p n i -> p (n i)").bitcast(I32))
+        nc.sync.dma_start(out=wb8_s[32 : 36, :], in_=wb8_scales[0].bitcast(I32)[4 : 8, :])
+        nc.sync.dma_start(out=wb8_s[64 : 68, :], in_=wb8_scales[0].bitcast(I32)[8 : 12, :])
+        nc.sync.dma_start(out=wb8_s[96 : 100, :], in_=wb8_scales[0].bitcast(I32)[12 : 16, :])
         nc.sync.dma_start(out=x0[1][:], in_=x0T[1 * P : 2 * P, :])
         nc.sync.dma_start(out=x0[2][:], in_=x0T[2 * P : 3 * P, :])
         nc.sync.dma_start(out=x0[3][:], in_=x0T[3 * P : 4 * P, :])
-        load_scales(nc.gpsimd, wb8_s, wb8_scales)
         with nc.allow_non_contiguous_dma(reason="one bias value to a partition"):
             nc.gpsimd.dma_start(out=b_col[:], in_=b.rearrange("(i p) -> p i", p=P))
+        nc.gpsimd.dma_start(out=wb8_s[0 : 4, :], in_=wb8_scales[0].bitcast(I32)[0 : 4, :])
 
-        nc.gpsimd.tensor_scalar(out=b_plus[:], in0=b_col[:], scalar1=1.0, scalar2=warm_out[:], op0=ALU.mult, op1=ALU.add)
+        nc.scalar.activation(out=b_plus[:], in_=b_col[:], func=ACT.Identity, bias=warm_out[:])
 
         dn_wp = keep.tile([P, 2 * R], U8, name="dn_wp", align_bytes=64)
         dn_sp = keep.tile([P, R], U8, name="dn_sp", align_bytes=64)
@@ -229,6 +232,7 @@ def tile_list_xcross_res_relu_kernel(
         pre_gather(0)
         for i in (1, 0):
             y_wb4(i, True, False)
+        for i in (1, 0):
             y_wb8(i, False, False)
         y_up(1, False, True)
         y_up(0, False, True)

@@ -33,7 +33,7 @@ def tile_list_xcross_res_relu_kernel(
         tab_w = keep.tile([P, T], I32, name="tab_w", align_bytes=64)
         tab_s = keep.tile([P, T // 4], I32, name="tab_s", align_bytes=64)
         dn_w = keep.tile([P, R // 2], I32, name="dn_w", align_bytes=64)
-        dn_s = keep.tile([P, R // 4], I32, name="dn_s", align_bytes=64)
+        dn_s = keep.tile([P, R // 4], I32, name="dn_s", tag="dealt_then_gathered", align_bytes=64)
         wb4_w = keep.tile([P, N // 2], I32, name="wb4_w", align_bytes=64)
         wb4_s = keep.tile([P, N // 4], I32, name="wb4_s", align_bytes=64)
         wb8_w = keep.tile([P, N], I32, name="wb8_w", align_bytes=64)
@@ -49,6 +49,9 @@ def tile_list_xcross_res_relu_kernel(
             for q in range(4):
                 queue.dma_start(out=plane[32 * q : 32 * q + 4, :], in_=rows[4 * q : 4 * q + 4, :])
 
+        def load_quadrant(queue, plane, src, q):
+            queue.dma_start(out=plane[32 * q : 32 * q + 4, :], in_=src[0].bitcast(I32)[4 * q : 4 * q + 4, :])
+
         warm_in = keep.tile([P, 1], F32, name="warm_in")
         warm_out = keep.tile([P, 1], F32, name="warm_out")
         nc.vector.memset(tab_s[:], 0)
@@ -56,31 +59,45 @@ def tile_list_xcross_res_relu_kernel(
         nc.vector.memset(dn_s[:], 0)
         nc.scalar.activation(out=warm_out[:], in_=warm_in[:], func=ACT.Copy, bias=1.0)
         nc.sync.dma_start(offsets[:], offs)
-        nc.sync.dma_start(out=tab_w[:], in_=tab_words[0].rearrange("p t i -> p (t i)").bitcast(I32))
-        load_scales(nc.sync, tab_s, tab_scales)
         nc.sync.dma_start(out=dn_w[:], in_=dn_words[0].bitcast(I32))
-        nc.sync.dma_start(out=up_raw[0][:], in_=up_view[:, :, 0 : 256])
-        load_scales(nc.sync, dn_s, dn_scales)
-        nc.sync.dma_start(out=wb4_w[:], in_=wb4_words[0].bitcast(I32))
-        nc.sync.dma_start(out=up_raw[1][:], in_=up_view[:, :, 256 : 512])
-        load_scales(nc.sync, wb4_s, wb4_scales)
+        load_quadrant(nc.sync, tab_s, tab_scales, 0)
+        load_quadrant(nc.sync, tab_s, tab_scales, 1)
+        load_quadrant(nc.sync, tab_s, tab_scales, 2)
+        load_quadrant(nc.sync, tab_s, tab_scales, 3)
+        nc.sync.dma_start(out=tab_w[:], in_=tab_words[0].rearrange("p t i -> p (t i)").bitcast(I32))
+        load_quadrant(nc.sync, dn_s, dn_scales, 0)
+        load_quadrant(nc.sync, dn_s, dn_scales, 1)
+        load_quadrant(nc.sync, dn_s, dn_scales, 2)
+        load_quadrant(nc.sync, dn_s, dn_scales, 3)
         nc.sync.dma_start(out=x0[0][:], in_=x0T[0 * P : 1 * P, :])
+        nc.sync.dma_start(out=up_raw[0][:], in_=up_view[:, :, 0 : 256])
+        nc.sync.dma_start(out=wb4_w[:], in_=wb4_words[0].bitcast(I32))
+        load_quadrant(nc.sync, wb4_s, wb4_scales, 2)
+        load_quadrant(nc.sync, wb4_s, wb4_scales, 3)
         nc.sync.dma_start(out=wb8_w[:], in_=wb8_words[0].rearrange("p n i -> p (n i)").bitcast(I32))
-        nc.sync.dma_start(out=wb8_s[32 : 36, :], in_=wb8_scales[0].bitcast(I32)[4 : 8, :])
-        nc.sync.dma_start(out=wb8_s[64 : 68, :], in_=wb8_scales[0].bitcast(I32)[8 : 12, :])
-        nc.sync.dma_start(out=wb8_s[96 : 100, :], in_=wb8_scales[0].bitcast(I32)[12 : 16, :])
+        nc.sync.dma_start(out=up_raw[1][:], in_=up_view[:, :, 256 : 512])
+        load_quadrant(nc.sync, wb8_s, wb8_scales, 0)
+        load_quadrant(nc.sync, wb8_s, wb8_scales, 1)
+        load_quadrant(nc.sync, wb8_s, wb8_scales, 2)
+        load_quadrant(nc.sync, wb8_s, wb8_scales, 3)
         nc.sync.dma_start(out=x0[1][:], in_=x0T[1 * P : 2 * P, :])
         nc.sync.dma_start(out=x0[2][:], in_=x0T[2 * P : 3 * P, :])
         nc.sync.dma_start(out=x0[3][:], in_=x0T[3 * P : 4 * P, :])
         with nc.allow_non_contiguous_dma(reason="one bias value to a partition"):
             nc.gpsimd.dma_start(out=b_col[:], in_=b.rearrange("(i p) -> p i", p=P))
-        nc.gpsimd.dma_start(out=wb8_s[0 : 4, :], in_=wb8_scales[0].bitcast(I32)[0 : 4, :])
-
+        load_quadrant(nc.gpsimd, wb4_s, wb4_scales, 0)
+        load_quadrant(nc.gpsimd, wb4_s, wb4_scales, 1)
         nc.scalar.activation(out=b_plus[:], in_=b_col[:], func=ACT.Identity, bias=warm_out[:])
 
         dn_wp = keep.tile([P, 2 * R], U8, name="dn_wp", align_bytes=64)
         dn_sp = keep.tile([P, R], U8, name="dn_sp", align_bytes=64)
-        v_w = keep.tile([P, J], U32, name="v_w", align_bytes=64)
+        LO = 128
+        v_lo = keep.tile([P, LO], U32, name="v_lo", align_bytes=64)
+        v_hi = keep.tile([P, J - LO], U32, name="v_hi", tag="dealt_then_gathered", align_bytes=64)
+
+        def v_cols(lo, hi):
+            return v_lo[:, lo:hi] if hi <= LO else v_hi[:, lo - LO : hi - LO]
+
         v_s = keep.tile([P, J], U8, name="v_s", align_bytes=64)
         up_b = keep.tile([P, N * PACK], BF16, name="up_b", align_bytes=64)
         up_w = keep.tile([P, N], U32, name="up_w", align_bytes=64)
@@ -100,7 +117,7 @@ def tile_list_xcross_res_relu_kernel(
             nc.vector.tensor_copy(out=v_s[:, lo:hi], in_=tab_s[:].bitcast(U8).indirect(listed(lo, hi)))
 
         def gather_w(lo, hi):
-            nc.vector.tensor_copy(out=v_w[:, lo:hi], in_=tab_w[:].bitcast(U32).indirect(listed(lo, hi)))
+            nc.vector.tensor_copy(out=v_cols(lo, hi), in_=tab_w[:].bitcast(U32).indirect(listed(lo, hi)))
 
         def perm_w():
             nc.vector.tensor_copy(
@@ -121,7 +138,7 @@ def tile_list_xcross_res_relu_kernel(
                     out=h_ps[c][:, t, :],
                     lhsT=dn_wp[:, 2 * t * P : 2 * (t + 1) * P].bitcast(FP4X4),
                     lhsT_scale=dn_sp[:, t * P : (t + 1) * P],
-                    rhs=v_w[:, cols].bitcast(FP8X4),
+                    rhs=v_cols(c * P, (c + 1) * P).bitcast(FP8X4),
                     rhs_scale=v_s[:, cols],
                     start=True,
                     stop=True,
@@ -174,26 +191,29 @@ def tile_list_xcross_res_relu_kernel(
             )
 
         def y_wb4(i, start, stop):
-            nc.tensor.matmul_mx(
-                out=y_ps[i][:],
-                lhsT=wb4_w[:].bitcast(U8)[:, 2 * i * P : 2 * (i + 1) * P].bitcast(FP4X4),
-                lhsT_scale=wb4_s[:].bitcast(U8)[:, i * P : (i + 1) * P],
-                rhs=v_w[:].bitcast(FP8X4),
-                rhs_scale=v_s[:],
-                start=start,
-                stop=stop,
-            )
+            for c in range(4):
+                cols = slice(c * P, (c + 1) * P)
+                nc.tensor.matmul_mx(
+                    out=y_ps[i][:, cols],
+                    lhsT=wb4_w[:].bitcast(U8)[:, 2 * i * P : 2 * (i + 1) * P].bitcast(FP4X4),
+                    lhsT_scale=wb4_s[:].bitcast(U8)[:, i * P : (i + 1) * P],
+                    rhs=v_cols(c * P, (c + 1) * P).bitcast(FP8X4),
+                    rhs_scale=v_s[:, cols],
+                    start=start and c == 0,
+                    stop=False,
+                )
 
         def y_wb8(i, start, stop):
-            nc.tensor.matmul_mx(
-                out=y_ps[i][:],
-                lhsT=wb8_w[:, i * P : (i + 1) * P].bitcast(FP8X4),
-                lhsT_scale=wb8_s[:].bitcast(U8)[:, i * P : (i + 1) * P],
-                rhs=v_w[:].bitcast(FP8X4),
-                rhs_scale=v_s[:],
-                start=start,
-                stop=stop,
-            )
+            for lo, hi in ((0, 128), (128, 256), (256, 512)):
+                nc.tensor.matmul_mx(
+                    out=y_ps[i][:, lo:hi],
+                    lhsT=wb8_w[:, i * P : (i + 1) * P].bitcast(FP8X4),
+                    lhsT_scale=wb8_s[:].bitcast(U8)[:, i * P : (i + 1) * P],
+                    rhs=v_cols(lo, hi).bitcast(FP8X4),
+                    rhs_scale=v_s[:, lo:hi],
+                    start=False,
+                    stop=False,
+                )
 
         def y_up(i, start, stop):
             nc.tensor.matmul_mx(
@@ -215,40 +235,44 @@ def tile_list_xcross_res_relu_kernel(
         def store(i, lo, hi):
             nc.sync.dma_start(out=out[i * P : (i + 1) * P, lo:hi], in_=res[i][:, lo:hi])
 
-        gather_s(0, 512)
+        def pre_part(i, lo, hi):
+            nc.vector.tensor_copy(out=y_sb[i][:, lo:hi], in_=x0[i][:].indirect(listed(lo, hi)))
+
         perm_w()
-        gather_w(0, 512)
+        gather_s(0, 512)
+        gather_w(0, P)
         perm_s()
-        up_cast(0, False)
-        for c in range(4):
+        h_mm(0)
+        for c in range(1, 4):
+            gather_w(c * P, (c + 1) * P)
             h_mm(c)
         for c in range(4):
             h_relu(c)
-        up_cast(1, True)
-        up_quant_all()
+        pre_gather(0)
         h_quant(0, 256)
+        up_cast(0, True)
         h_quant(256, 384)
         h_quant(384, 512)
-        pre_gather(0)
-        for i in (1, 0):
+        up_quant(0)
+        up_cast(1, True)
+        up_quant(1)
+        for i in (0, 1):
             y_wb4(i, True, False)
-        for i in (1, 0):
             y_wb8(i, False, False)
-        y_up(1, False, True)
         y_up(0, False, True)
+        y_up(1, False, True)
         for i in (2, 3):
             y_wb4(i, True, False)
             y_wb8(i, False, False)
-            y_up(i, False, True)
-        y_out(1, 0, J)
+        y_up(2, False, True)
+        y_up(3, False, True)
         cross_psum(0)
         store(0, 0, J)
-        cross(1, 0, J)
-        store(1, 0, J)
-        y_out(2, 0, J)
-        cross(2, 0, J)
-        store(2, 0, J)
+        for i in (1, 2):
+            y_out(i, 0, J)
+            cross(i, 0, J)
+            store(i, 0, J)
+        y_out(3, 0, J)
         for lo in (0, 256):
-            y_out(3, lo, lo + 256)
             cross(3, lo, lo + 256)
             store(3, lo, lo + 256)

@@ -50,7 +50,7 @@ def tile_list_xcross_res_relu_kernel(
                 queue.dma_start(out=plane[32 * q : 32 * q + 4, :], in_=rows[4 * q : 4 * q + 4, :])
 
         def load_quadrant(queue, plane, src, q):
-            queue.dma_start(out=plane[32 * q : 32 * q + 4, :], in_=src[0].bitcast(I32)[4 * q : 4 * q + 4, :])
+            queue.dma_start(out=plane[q : P : 32, :], in_=src[0].bitcast(I32)[q : 16 : 4, :])
 
         warm_in = keep.tile([P, 1], F32, name="warm_in")
         warm_out = keep.tile([P, 1], F32, name="warm_out")

@@ -91,13 +91,8 @@ def tile_list_xcross_res_relu_kernel(
 
         dn_wp = keep.tile([P, 2 * R], U8, name="dn_wp", align_bytes=64)
         dn_sp = keep.tile([P, R], U8, name="dn_sp", align_bytes=64)
-        LO = 128
-        v_lo = keep.tile([P, LO], U32, name="v_lo", align_bytes=64)
-        v_hi = keep.tile([P, J - LO], U32, name="v_hi", tag="dealt_then_gathered", align_bytes=64)
-
-        def v_cols(lo, hi):
-            return v_lo[:, lo:hi] if hi <= LO else v_hi[:, lo - LO : hi - LO]
-
+        v_first = keep.tile([P, P], U32, name="v_first", align_bytes=64)
+        v_w = keep.tile([P, J], U32, name="v_w", tag="dealt_then_gathered", align_bytes=64)
         v_s = keep.tile([P, J], U8, name="v_s", align_bytes=64)
         up_b = keep.tile([P, N * PACK], BF16, name="up_b", align_bytes=64)
         up_w = keep.tile([P, N], U32, name="up_w", align_bytes=64)
@@ -117,7 +112,7 @@ def tile_list_xcross_res_relu_kernel(
             nc.vector.tensor_copy(out=v_s[:, lo:hi], in_=tab_s[:].bitcast(U8).indirect(listed(lo, hi)))
 
         def gather_w(lo, hi):
-            nc.vector.tensor_copy(out=v_cols(lo, hi), in_=tab_w[:].bitcast(U32).indirect(listed(lo, hi)))
+            nc.vector.tensor_copy(out=v_w[:, lo:hi], in_=tab_w[:].bitcast(U32).indirect(listed(lo, hi)))
 
         def perm_w():
             nc.vector.tensor_copy(
@@ -138,7 +133,7 @@ def tile_list_xcross_res_relu_kernel(
                     out=h_ps[c][:, t, :],
                     lhsT=dn_wp[:, 2 * t * P : 2 * (t + 1) * P].bitcast(FP4X4),
                     lhsT_scale=dn_sp[:, t * P : (t + 1) * P],
-                    rhs=v_cols(c * P, (c + 1) * P).bitcast(FP8X4),
+                    rhs=(v_first[:] if c == 0 else v_w[:, cols]).bitcast(FP8X4),
                     rhs_scale=v_s[:, cols],
                     start=True,
                     stop=True,
@@ -191,29 +186,26 @@ def tile_list_xcross_res_relu_kernel(
             )
 
         def y_wb4(i, start, stop):
-            for c in range(4):
-                cols = slice(c * P, (c + 1) * P)
-                nc.tensor.matmul_mx(
-                    out=y_ps[i][:, cols],
-                    lhsT=wb4_w[:].bitcast(U8)[:, 2 * i * P : 2 * (i + 1) * P].bitcast(FP4X4),
-                    lhsT_scale=wb4_s[:].bitcast(U8)[:, i * P : (i + 1) * P],
-                    rhs=v_cols(c * P, (c + 1) * P).bitcast(FP8X4),
-                    rhs_scale=v_s[:, cols],
-                    start=start and c == 0,
-                    stop=False,
-                )
+            nc.tensor.matmul_mx(
+                out=y_ps[i][:],
+                lhsT=wb4_w[:].bitcast(U8)[:, 2 * i * P : 2 * (i + 1) * P].bitcast(FP4X4),
+                lhsT_scale=wb4_s[:].bitcast(U8)[:, i * P : (i + 1) * P],
+                rhs=v_w[:].bitcast(FP8X4),
+                rhs_scale=v_s[:],
+                start=start,
+                stop=stop,
+            )
 
         def y_wb8(i, start, stop):
-            for lo, hi in ((0, 128), (128, 256), (256, 512)):
-                nc.tensor.matmul_mx(
-                    out=y_ps[i][:, lo:hi],
-                    lhsT=wb8_w[:, i * P : (i + 1) * P].bitcast(FP8X4),
-                    lhsT_scale=wb8_s[:].bitcast(U8)[:, i * P : (i + 1) * P],
-                    rhs=v_cols(lo, hi).bitcast(FP8X4),
-                    rhs_scale=v_s[:, lo:hi],
-                    start=False,
-                    stop=False,
-                )
+            nc.tensor.matmul_mx(
+                out=y_ps[i][:],
+                lhsT=wb8_w[:, i * P : (i + 1) * P].bitcast(FP8X4),
+                lhsT_scale=wb8_s[:].bitcast(U8)[:, i * P : (i + 1) * P],
+                rhs=v_w[:].bitcast(FP8X4),
+                rhs_scale=v_s[:],
+                start=start,
+                stop=stop,
+            )
 
         def y_up(i, start, stop):
             nc.tensor.matmul_mx(
@@ -235,17 +227,17 @@ def tile_list_xcross_res_relu_kernel(
         def store(i, lo, hi):
             nc.sync.dma_start(out=out[i * P : (i + 1) * P, lo:hi], in_=res[i][:, lo:hi])
 
-        def pre_part(i, lo, hi):
-            nc.vector.tensor_copy(out=y_sb[i][:, lo:hi], in_=x0[i][:].indirect(listed(lo, hi)))
-
         perm_w()
         gather_s(0, 512)
-        gather_w(0, P)
+        nc.vector.tensor_copy(out=v_first[:], in_=tab_w[:].bitcast(U32).indirect(listed(0, P)))
         perm_s()
         h_mm(0)
-        for c in range(1, 4):
-            gather_w(c * P, (c + 1) * P)
-            h_mm(c)
+        gather_w(128, 256)
+        h_mm(1)
+        gather_w(256, 512)
+        h_mm(2)
+        h_mm(3)
+        gather_w(0, 128)
         for c in range(4):
             h_relu(c)
         pre_gather(0)
@@ -254,7 +246,7 @@ def tile_list_xcross_res_relu_kernel(
         h_quant(256, 384)
         h_quant(384, 512)
         up_quant(0)
-        up_cast(1, True)
+        up_cast(1, False)
         up_quant(1)
         for i in (0, 1):
             y_wb4(i, True, False)
@@ -262,10 +254,9 @@ def tile_list_xcross_res_relu_kernel(
         y_up(0, False, True)
         y_up(1, False, True)
         for i in (2, 3):
-            y_wb4(i, True, False)
-            y_wb8(i, False, False)
-        y_up(2, False, True)
-        y_up(3, False, True)
+            y_wb8(i, True, False)
+            y_wb4(i, False, False)
+            y_up(i, False, True)
         cross_psum(0)
         store(0, 0, J)
         for i in (1, 2):

@@ -72,9 +72,11 @@ def tile_list_xcross_res_relu_kernel(
         nc.sync.dma_start(out=x0[0][:], in_=x0T[0 * P : 1 * P, :])
         nc.sync.dma_start(out=up_raw[0][:], in_=up_view[:, :, 0 : 256])
         nc.sync.dma_start(out=wb4_w[:], in_=wb4_words[0].bitcast(I32))
+        load_quadrant(nc.sync, wb4_s, wb4_scales, 0)
+        load_quadrant(nc.sync, wb4_s, wb4_scales, 1)
+        nc.sync.dma_start(out=wb8_w[:], in_=wb8_words[0].rearrange("p n i -> p (n i)").bitcast(I32))
         load_quadrant(nc.sync, wb4_s, wb4_scales, 2)
         load_quadrant(nc.sync, wb4_s, wb4_scales, 3)
-        nc.sync.dma_start(out=wb8_w[:], in_=wb8_words[0].rearrange("p n i -> p (n i)").bitcast(I32))
         nc.sync.dma_start(out=up_raw[1][:], in_=up_view[:, :, 256 : 512])
         load_quadrant(nc.sync, wb8_s, wb8_scales, 0)
         load_quadrant(nc.sync, wb8_s, wb8_scales, 1)
@@ -85,8 +87,6 @@ def tile_list_xcross_res_relu_kernel(
         nc.sync.dma_start(out=x0[3][:], in_=x0T[3 * P : 4 * P, :])
         with nc.allow_non_contiguous_dma(reason="one bias value to a partition"):
             nc.gpsimd.dma_start(out=b_col[:], in_=b.rearrange("(i p) -> p i", p=P))
-        load_quadrant(nc.gpsimd, wb4_s, wb4_scales, 0)
-        load_quadrant(nc.gpsimd, wb4_s, wb4_scales, 1)
         nc.scalar.activation(out=b_plus[:], in_=b_col[:], func=ACT.Identity, bias=warm_out[:])
 
         dn_wp = keep.tile([P, 2 * R], U8, name="dn_wp", align_bytes=64)

@@ -1,6 +1,7 @@
 from contextlib import ExitStack
 
 import concourse.mybir as mybir
+from concourse.masks import make_identity
 
 K, R, N, T, J = 512, 512, 512, 1024, 512
 FLOPS = 2 * J * (K * R + 2 * K * N + R * N)
@@ -40,7 +41,9 @@ def tile_list_xcross_res_relu_kernel(
         wb8_s = keep.tile([P, N // 4], I32, name="wb8_s", align_bytes=64)
         up_raw = [keep.tile([P, PACK, N // 2], F32, name="up_raw%d" % u) for u in range(2)]
         x0 = [keep.tile([P, T], F32, name="x0_%d" % i) for i in range(4)]
-        b_col = keep.tile([P, 4], F32, name="b_col")
+        b_rows = keep.tile([P, P], F32, name="b_rows")
+        ident = keep.tile([P, P], F32, name="ident")
+        b_ps = psum.tile([P, P], F32, name="b_ps", tag="y_ps3")
         b_plus = keep.tile([P, 4], F32, name="b_plus")
         up_view = upw.rearrange("(p i) n -> p i n", i=PACK)
 
@@ -85,9 +88,11 @@ def tile_list_xcross_res_relu_kernel(
         nc.sync.dma_start(out=x0[1][:], in_=x0T[1 * P : 2 * P, :])
         nc.sync.dma_start(out=x0[2][:], in_=x0T[2 * P : 3 * P, :])
         nc.sync.dma_start(out=x0[3][:], in_=x0T[3 * P : 4 * P, :])
-        with nc.allow_non_contiguous_dma(reason="one bias value to a partition"):
-            nc.gpsimd.dma_start(out=b_col[:], in_=b.rearrange("(i p) -> p i", p=P))
-        nc.scalar.activation(out=b_plus[:], in_=b_col[:], func=ACT.Identity, bias=warm_out[:])
+        nc.gpsimd.memset(b_rows[:], 0.0)
+        nc.gpsimd.dma_start(out=b_rows[0:4, :], in_=b.rearrange("(i p) -> i p", p=P))
+        make_identity(nc, ident[:])
+        nc.tensor.transpose(b_ps[:], b_rows[:], ident[:])
+        nc.scalar.activation(out=b_plus[:], in_=b_ps[:, 0:4], func=ACT.Identity, bias=warm_out[:])
 
         dn_wp = keep.tile([P, 2 * R], U8, name="dn_wp", align_bytes=64)
         dn_sp = keep.tile([P, R], U8, name="dn_sp", align_bytes=64)
@@ -101,7 +106,7 @@ def tile_list_xcross_res_relu_kernel(
         h_w = keep.tile([P, J], U32, name="h_w", align_bytes=64)
         h_s = keep.tile([P, J], U8, name="h_s", align_bytes=64)
         h_ps = [psum.tile([P, PACK, P], F32, name="h_ps%d" % c) for c in range(4)]
-        y_ps = [psum.tile([P, J], F32, name="y_ps%d" % i) for i in range(4)]
+        y_ps = [psum.tile([P, J], F32, name="y_ps%d" % i, tag="y_ps%d" % i) for i in range(4)]
         y_sb = [keep.tile([P, J], F32, name="y_sb%d" % i) for i in range(4)]
         res = [keep.tile([P, J], F32, name="res%d" % i) for i in range(4)]
 

@@ -39,8 +39,8 @@ def tile_list_xcross_res_relu_kernel(
         wb4_s = keep.tile([P, N // 4], I32, name="wb4_s", align_bytes=64)
         wb8_w = keep.tile([P, N], I32, name="wb8_w", align_bytes=64)
         wb8_s = keep.tile([P, N // 4], I32, name="wb8_s", align_bytes=64)
-        up_raw = [keep.tile([P, PACK, N // 2], F32, name="up_raw%d" % u) for u in range(2)]
-        x0 = [keep.tile([P, T], F32, name="x0_%d" % i) for i in range(4)]
+        up_raw = keep.tile([P, PACK, N], F32, name="up_raw")
+        x0 = [keep.tile([P, T], F32, name="x0_%d" % i, tag="x0_%d" % i, align_bytes=64) for i in range(4)]
         b_rows = keep.tile([P, P], F32, name="b_rows")
         ident = keep.tile([P, P], F32, name="ident")
         b_ps = psum.tile([P, P], F32, name="b_ps", tag="y_ps3")
@@ -60,6 +60,7 @@ def tile_list_xcross_res_relu_kernel(
         nc.vector.memset(tab_s[:], 0)
         nc.vector.memset(warm_in[:], 0.0)
         nc.vector.memset(dn_s[:], 0)
+        nc.gpsimd.memset(b_rows[:], 0.0)
         nc.scalar.activation(out=warm_out[:], in_=warm_in[:], func=ACT.Copy, bias=1.0)
         nc.sync.dma_start(offsets[:], offs)
         nc.sync.dma_start(out=dn_w[:], in_=dn_words[0].bitcast(I32))
@@ -72,39 +73,44 @@ def tile_list_xcross_res_relu_kernel(
         load_quadrant(nc.sync, dn_s, dn_scales, 1)
         load_quadrant(nc.sync, dn_s, dn_scales, 2)
         load_quadrant(nc.sync, dn_s, dn_scales, 3)
-        nc.sync.dma_start(out=x0[0][:], in_=x0T[0 * P : 1 * P, :])
-        nc.sync.dma_start(out=up_raw[0][:], in_=up_view[:, :, 0 : 256])
-        nc.sync.dma_start(out=wb4_w[:], in_=wb4_words[0].bitcast(I32))
-        load_quadrant(nc.sync, wb4_s, wb4_scales, 0)
-        load_quadrant(nc.sync, wb4_s, wb4_scales, 1)
-        nc.sync.dma_start(out=wb8_w[:], in_=wb8_words[0].rearrange("p n i -> p (n i)").bitcast(I32))
-        load_quadrant(nc.sync, wb4_s, wb4_scales, 2)
-        load_quadrant(nc.sync, wb4_s, wb4_scales, 3)
-        nc.sync.dma_start(out=up_raw[1][:], in_=up_view[:, :, 256 : 512])
+        nc.sync.dma_start(out=up_raw[:, 0:2, :], in_=up_view[:, 0:2, :])
         load_quadrant(nc.sync, wb8_s, wb8_scales, 0)
+        nc.sync.dma_start(out=up_raw[:, 2:4, :], in_=up_view[:, 2:4, :])
         load_quadrant(nc.sync, wb8_s, wb8_scales, 1)
         load_quadrant(nc.sync, wb8_s, wb8_scales, 2)
         load_quadrant(nc.sync, wb8_s, wb8_scales, 3)
+        nc.sync.dma_start(out=wb8_w[:], in_=wb8_words[0].rearrange("p n i -> p (n i)").bitcast(I32))
+        nc.sync.dma_start(out=wb4_w[:], in_=wb4_words[0].bitcast(I32))
+        load_quadrant(nc.sync, wb4_s, wb4_scales, 0)
+        nc.sync.dma_start(out=x0[0][:], in_=x0T[0 * P : 1 * P, :])
+        load_quadrant(nc.sync, wb4_s, wb4_scales, 1)
+        load_quadrant(nc.sync, wb4_s, wb4_scales, 2)
+        load_quadrant(nc.sync, wb4_s, wb4_scales, 3)
         nc.sync.dma_start(out=x0[1][:], in_=x0T[1 * P : 2 * P, :])
         nc.sync.dma_start(out=x0[2][:], in_=x0T[2 * P : 3 * P, :])
         nc.sync.dma_start(out=x0[3][:], in_=x0T[3 * P : 4 * P, :])
-        nc.gpsimd.memset(b_rows[:], 0.0)
         nc.gpsimd.dma_start(out=b_rows[0:4, :], in_=b.rearrange("(i p) -> i p", p=P))
         make_identity(nc, ident[:])
         nc.tensor.transpose(b_ps[:], b_rows[:], ident[:])
         nc.scalar.activation(out=b_plus[:], in_=b_ps[:, 0:4], func=ACT.Identity, bias=warm_out[:])
 
-        dn_wp = keep.tile([P, 2 * R], U8, name="dn_wp", align_bytes=64)
+        dn_wp = keep.tile([P, 2 * R], U8, name="dn_wp", tag="dealt_then_cast", align_bytes=64)
         dn_sp = keep.tile([P, R], U8, name="dn_sp", align_bytes=64)
         v_first = keep.tile([P, P], U32, name="v_first", align_bytes=64)
         v_w = keep.tile([P, J], U32, name="v_w", tag="dealt_then_gathered", align_bytes=64)
         v_s = keep.tile([P, J], U8, name="v_s", align_bytes=64)
-        up_b = keep.tile([P, N * PACK], BF16, name="up_b", align_bytes=64)
-        up_w = keep.tile([P, N], U32, name="up_w", align_bytes=64)
+        up_b = [
+            keep.tile([P, N * PACK // 2], BF16, name="up_b0", tag="cast_then_h_scales", align_bytes=64),
+            keep.tile([P, N * PACK // 2], BF16, name="up_b1", tag="dealt_then_cast", align_bytes=64),
+        ]
+        up_w = [
+            keep.tile([P, N // 2], U32, name="up_w0", align_bytes=64),
+            keep.tile([P, N // 2], U32, name="up_w1", tag="x0_0", align_bytes=64),
+        ]
         up_s = keep.tile([P, N], U8, name="up_s", align_bytes=64)
         h_b = keep.tile([P, J * PACK], BF16, name="h_b", align_bytes=64)
         h_w = keep.tile([P, J], U32, name="h_w", align_bytes=64)
-        h_s = keep.tile([P, J], U8, name="h_s", align_bytes=64)
+        h_s = keep.tile([P, J], U8, name="h_s", tag="cast_then_h_scales", align_bytes=64)
         h_ps = [psum.tile([P, PACK, P], F32, name="h_ps%d" % c) for c in range(4)]
         y_ps = [psum.tile([P, J], F32, name="y_ps%d" % i, tag="y_ps%d" % i) for i in range(4)]
         y_sb = [keep.tile([P, J], F32, name="y_sb%d" % i) for i in range(4)]
@@ -165,8 +171,8 @@ def tile_list_xcross_res_relu_kernel(
 
         def up_cast(u, on_vector):
             half = N // 2
-            dst = up_b[:, u * half * PACK : (u + 1) * half * PACK].rearrange("p (c e i) -> p c i e", e=4, i=PACK)
-            src = up_raw[u][:].rearrange("p i (c e) -> p c i e", e=4)
+            dst = up_b[u][:].rearrange("p (c e i) -> p c i e", e=4, i=PACK)
+            src = up_raw[:, :, u * half : (u + 1) * half].rearrange("p i (c e) -> p c i e", e=4)
             if on_vector:
                 nc.vector.tensor_copy(out=dst, in_=src)
             else:
@@ -176,11 +182,8 @@ def tile_list_xcross_res_relu_kernel(
             half = N // 2
             cols = slice(u * half, (u + 1) * half)
             nc.vector.quantize_mx(
-                out=up_w[:, cols].bitcast(FP8X4), scales=up_s[:, cols], in_=up_b[:, u * half * PACK : (u + 1) * half * PACK]
+                out=up_w[u][:].bitcast(FP8X4), scales=up_s[:, cols], in_=up_b[u][:]
             )
-
-        def up_quant_all():
-            nc.vector.quantize_mx(out=up_w[:].bitcast(FP8X4), scales=up_s[:], in_=up_b[:])
 
         def pre_gather(i):
             nc.vector.tensor_copy(out=y_sb[i][:], in_=x0[i][:].indirect(offsets[:]))
@@ -215,7 +218,7 @@ def tile_list_xcross_res_relu_kernel(
         def y_up(i, start, stop):
             nc.tensor.matmul_mx(
                 out=y_ps[i][:],
-                lhsT=up_w[:, i * P : (i + 1) * P].bitcast(FP8X4),
+                lhsT=up_w[i // 2][:, i % 2 * P : (i % 2 + 1) * P].bitcast(FP8X4),
                 lhsT_scale=up_s[:, i * P : (i + 1) * P],
                 rhs=h_w[:].bitcast(FP8X4),
                 rhs_scale=h_s[:],
@@ -245,21 +248,21 @@ def tile_list_xcross_res_relu_kernel(
         gather_w(0, 128)
         for c in range(4):
             h_relu(c)
-        pre_gather(0)
-        h_quant(0, 256)
         up_cast(0, True)
+        h_quant(0, 256)
+        up_quant(0)
         h_quant(256, 384)
         h_quant(384, 512)
-        up_quant(0)
         up_cast(1, False)
+        pre_gather(0)
         up_quant(1)
-        for i in (0, 1):
-            y_wb4(i, True, False)
-            y_wb8(i, False, False)
-        y_up(0, False, True)
-        y_up(1, False, True)
-        for i in (2, 3):
+        for i in range(4):
             y_wb8(i, True, False)
+        for i in (0, 1):
+            y_up(i, False, False)
+        for i in (0, 1):
+            y_wb4(i, False, True)
+        for i in (2, 3):
             y_wb4(i, False, False)
             y_up(i, False, True)
         cross_psum(0)

@@ -100,7 +100,8 @@ def tile_list_xcross_res_relu_kernel(
         v_w = keep.tile([P, J], U32, name="v_w", tag="dealt_then_gathered", align_bytes=64)
         v_s = keep.tile([P, J], U8, name="v_s", align_bytes=64)
         up_b = [
-            keep.tile([P, N * PACK // 2], BF16, name="up_b0", tag="cast_then_h_scales", align_bytes=64),
+            keep.tile([P, P * PACK], BF16, name="up_b0", tag="cast_then_h_scales", align_bytes=64),
+            keep.tile([P, P * PACK], BF16, name="up_b0b", align_bytes=64),
             keep.tile([P, N * PACK // 2], BF16, name="up_b1", tag="dealt_then_cast", align_bytes=64),
         ]
         up_w = [
@@ -169,20 +170,22 @@ def tile_list_xcross_res_relu_kernel(
         def h_quant(lo, hi):
             nc.vector.quantize_mx(out=h_w[:, lo:hi].bitcast(FP8X4), scales=h_s[:, lo:hi], in_=h_b[:, lo * PACK : hi * PACK])
 
+        up_cols = ((0, P), (P, 2 * P), (2 * P, N))
+
         def up_cast(u, on_vector):
-            half = N // 2
+            lo, hi = up_cols[u]
             dst = up_b[u][:].rearrange("p (c e i) -> p c i e", e=4, i=PACK)
-            src = up_raw[:, :, u * half : (u + 1) * half].rearrange("p i (c e) -> p c i e", e=4)
+            src = up_raw[:, :, lo:hi].rearrange("p i (c e) -> p c i e", e=4)
             if on_vector:
                 nc.vector.tensor_copy(out=dst, in_=src)
             else:
                 nc.scalar.copy(out=dst, in_=src)
 
         def up_quant(u):
-            half = N // 2
-            cols = slice(u * half, (u + 1) * half)
+            lo, hi = up_cols[u]
+            base = lo // 256 * 256
             nc.vector.quantize_mx(
-                out=up_w[u][:].bitcast(FP8X4), scales=up_s[:, cols], in_=up_b[u][:]
+                out=up_w[lo // 256][:, lo - base : hi - base].bitcast(FP8X4), scales=up_s[:, lo:hi], in_=up_b[u][:]
             )
 
         def pre_gather(i):
@@ -249,18 +252,20 @@ def tile_list_xcross_res_relu_kernel(
         for c in range(4):
             h_relu(c)
         up_cast(0, True)
-        h_quant(0, 256)
+        up_cast(1, True)
         up_quant(0)
+        up_quant(1)
+        h_quant(0, 256)
         h_quant(256, 384)
         h_quant(384, 512)
-        up_cast(1, False)
+        up_cast(2, False)
         pre_gather(0)
-        up_quant(1)
+        up_quant(2)
         for i in range(4):
             y_wb8(i, True, False)
-        for i in (0, 1):
+        for i in (1, 0):
             y_up(i, False, False)
-        for i in (0, 1):
+        for i in (1, 0):
             y_wb4(i, False, True)
         for i in (2, 3):
             y_wb4(i, False, False)
@@ -272,6 +277,6 @@ def tile_list_xcross_res_relu_kernel(
             cross(i, 0, J)
             store(i, 0, J)
         y_out(3, 0, J)
-        for lo in (0, 256):
-            cross(3, lo, lo + 256)
-            store(3, lo, lo + 256)
+        for lo, hi in ((0, 256), (256, 512)):
+            cross(3, lo, hi)
+            store(3, lo, hi)

@@ -80,9 +80,9 @@ def tile_list_xcross_res_relu_kernel(
         load_quadrant(nc.sync, wb8_s, wb8_scales, 2)
         load_quadrant(nc.sync, wb8_s, wb8_scales, 3)
         nc.sync.dma_start(out=wb8_w[:], in_=wb8_words[0].rearrange("p n i -> p (n i)").bitcast(I32))
+        nc.sync.dma_start(out=x0[0][:], in_=x0T[0 * P : 1 * P, :])
         nc.sync.dma_start(out=wb4_w[:], in_=wb4_words[0].bitcast(I32))
         load_quadrant(nc.sync, wb4_s, wb4_scales, 0)
-        nc.sync.dma_start(out=x0[0][:], in_=x0T[0 * P : 1 * P, :])
         load_quadrant(nc.sync, wb4_s, wb4_scales, 1)
         load_quadrant(nc.sync, wb4_s, wb4_scales, 2)
         load_quadrant(nc.sync, wb4_s, wb4_scales, 3)

@@ -39,7 +39,7 @@ def tile_list_xcross_res_relu_kernel(
         wb4_s = keep.tile([P, N // 4], I32, name="wb4_s", align_bytes=64)
         wb8_w = keep.tile([P, N], I32, name="wb8_w", align_bytes=64)
         wb8_s = keep.tile([P, N // 4], I32, name="wb8_s", align_bytes=64)
-        up_raw = keep.tile([P, PACK, N], F32, name="up_raw")
+        up_raw = [keep.tile([P, PACK, N // 2], F32, name="up_raw%d" % u) for u in range(2)]
         x0 = [keep.tile([P, T], F32, name="x0_%d" % i, tag="x0_%d" % i, align_bytes=64) for i in range(4)]
         b_rows = keep.tile([P, P], F32, name="b_rows")
         ident = keep.tile([P, P], F32, name="ident")
@@ -73,9 +73,9 @@ def tile_list_xcross_res_relu_kernel(
         load_quadrant(nc.sync, dn_s, dn_scales, 1)
         load_quadrant(nc.sync, dn_s, dn_scales, 2)
         load_quadrant(nc.sync, dn_s, dn_scales, 3)
-        nc.sync.dma_start(out=up_raw[:, 0:2, :], in_=up_view[:, 0:2, :])
+        nc.sync.dma_start(out=up_raw[0][:], in_=up_view[:, :, 0 : N // 2])
         load_quadrant(nc.sync, wb8_s, wb8_scales, 0)
-        nc.sync.dma_start(out=up_raw[:, 2:4, :], in_=up_view[:, 2:4, :])
+        nc.sync.dma_start(out=up_raw[1][:], in_=up_view[:, :, N // 2 : N])
         load_quadrant(nc.sync, wb8_s, wb8_scales, 1)
         load_quadrant(nc.sync, wb8_s, wb8_scales, 2)
         load_quadrant(nc.sync, wb8_s, wb8_scales, 3)
@@ -175,7 +175,7 @@ def tile_list_xcross_res_relu_kernel(
         def up_cast(u, on_vector):
             lo, hi = up_cols[u]
             dst = up_b[u][:].rearrange("p (c e i) -> p c i e", e=4, i=PACK)
-            src = up_raw[:, :, lo:hi].rearrange("p i (c e) -> p c i e", e=4)
+            src = up_raw[lo // 256][:, :, lo % 256 : lo % 256 + hi - lo].rearrange("p i (c e) -> p c i e", e=4)
             if on_vector:
                 nc.vector.tensor_copy(out=dst, in_=src)
             else:

@@ -20,6 +20,7 @@ ALU = mybir.AluOpType
 P = 128
 PACK = 4
 LIST_ROWS = 16
+HALF = J // 2
 
 
 def tile_list_xcross_res_relu_kernel(
@@ -32,9 +33,9 @@ def tile_list_xcross_res_relu_kernel(
 
         offsets = keep.tile([P, J // LIST_ROWS], U16, name="offsets")
         tab_w = keep.tile([P, T], I32, name="tab_w", align_bytes=64)
-        tab_s = keep.tile([P, T // 4], I32, name="tab_s", align_bytes=64)
+        tab_s = keep.tile([P, T // 4], I32, name="tab_s", tag="scales_then_words", align_bytes=64)
         dn_w = keep.tile([P, R // 2], I32, name="dn_w", align_bytes=64)
-        dn_s = keep.tile([P, R // 4], I32, name="dn_s", tag="dealt_then_gathered", align_bytes=64)
+        dn_s = keep.tile([P, R // 4], I32, name="dn_s", align_bytes=64)
         wb4_w = keep.tile([P, N // 2], I32, name="wb4_w", align_bytes=64)
         wb4_s = keep.tile([P, N // 4], I32, name="wb4_s", align_bytes=64)
         wb8_w = keep.tile([P, N], I32, name="wb8_w", align_bytes=64)
@@ -47,10 +48,9 @@ def tile_list_xcross_res_relu_kernel(
         b_plus = keep.tile([P, 4], F32, name="b_plus")
         up_view = upw.rearrange("(p i) n -> p i n", i=PACK)
 
-        def load_scales(queue, plane, src):
-            rows = src[0].bitcast(I32)
-            for q in range(4):
-                queue.dma_start(out=plane[32 * q : 32 * q + 4, :], in_=rows[4 * q : 4 * q + 4, :])
+        def fill_quadrant(queue, plane, src, q):
+            rows = src[0].bitcast(I32)[4 * q : 4 * q + 4, :]
+            queue.dma_start(out=plane[32 * q : 32 * q + 32, :], in_=rows.partition_broadcast(8))
 
         def load_quadrant(queue, plane, src, q):
             queue.dma_start(out=plane[q : P : 32, :], in_=src[0].bitcast(I32)[q : 16 : 4, :])
@@ -59,62 +59,64 @@ def tile_list_xcross_res_relu_kernel(
         warm_out = keep.tile([P, 1], F32, name="warm_out")
         nc.vector.memset(tab_s[:], 0)
         nc.vector.memset(warm_in[:], 0.0)
-        nc.vector.memset(dn_s[:], 0)
         nc.gpsimd.memset(b_rows[:], 0.0)
-        nc.scalar.activation(out=warm_out[:], in_=warm_in[:], func=ACT.Copy, bias=1.0)
         nc.sync.dma_start(offsets[:], offs)
+        fill_quadrant(nc.scalar, dn_s, dn_scales, 0)
         nc.sync.dma_start(out=dn_w[:], in_=dn_words[0].bitcast(I32))
-        load_quadrant(nc.sync, tab_s, tab_scales, 0)
+        fill_quadrant(nc.scalar, dn_s, dn_scales, 1)
+        fill_quadrant(nc.sync, dn_s, dn_scales, 3)
+        fill_quadrant(nc.scalar, dn_s, dn_scales, 2)
+        nc.sync.dma_start(out=tab_w[:], in_=tab_words[0].rearrange("p t i -> p (t i)").bitcast(I32))
+        load_quadrant(nc.scalar, tab_s, tab_scales, 0)
+        nc.scalar.activation(out=warm_out[:], in_=warm_in[:], func=ACT.Copy, bias=1.0)
         load_quadrant(nc.sync, tab_s, tab_scales, 1)
         load_quadrant(nc.sync, tab_s, tab_scales, 2)
         load_quadrant(nc.sync, tab_s, tab_scales, 3)
-        nc.sync.dma_start(out=tab_w[:], in_=tab_words[0].rearrange("p t i -> p (t i)").bitcast(I32))
-        load_quadrant(nc.sync, dn_s, dn_scales, 0)
-        load_quadrant(nc.sync, dn_s, dn_scales, 1)
-        load_quadrant(nc.sync, dn_s, dn_scales, 2)
-        load_quadrant(nc.sync, dn_s, dn_scales, 3)
         nc.sync.dma_start(out=up_raw[0][:], in_=up_view[:, :, 0 : N // 2])
-        load_quadrant(nc.sync, wb8_s, wb8_scales, 0)
-        nc.sync.dma_start(out=up_raw[1][:], in_=up_view[:, :, N // 2 : N])
-        load_quadrant(nc.sync, wb8_s, wb8_scales, 1)
-        load_quadrant(nc.sync, wb8_s, wb8_scales, 2)
-        load_quadrant(nc.sync, wb8_s, wb8_scales, 3)
         nc.sync.dma_start(out=wb8_w[:], in_=wb8_words[0].rearrange("p n i -> p (n i)").bitcast(I32))
+        for q in range(4):
+            load_quadrant(nc.sync, wb4_s, wb4_scales, q)
         nc.sync.dma_start(out=x0[0][:], in_=x0T[0 * P : 1 * P, :])
         nc.sync.dma_start(out=wb4_w[:], in_=wb4_words[0].bitcast(I32))
-        load_quadrant(nc.sync, wb4_s, wb4_scales, 0)
-        load_quadrant(nc.sync, wb4_s, wb4_scales, 1)
-        load_quadrant(nc.sync, wb4_s, wb4_scales, 2)
-        load_quadrant(nc.sync, wb4_s, wb4_scales, 3)
+        nc.sync.dma_start(out=up_raw[1][:], in_=up_view[:, :, N // 2 : N])
+        for q in range(4):
+            load_quadrant(nc.sync, wb8_s, wb8_scales, q)
         nc.sync.dma_start(out=x0[1][:], in_=x0T[1 * P : 2 * P, :])
         nc.sync.dma_start(out=x0[2][:], in_=x0T[2 * P : 3 * P, :])
         nc.sync.dma_start(out=x0[3][:], in_=x0T[3 * P : 4 * P, :])
         nc.gpsimd.dma_start(out=b_rows[0:4, :], in_=b.rearrange("(i p) -> i p", p=P))
         make_identity(nc, ident[:])
         nc.tensor.transpose(b_ps[:], b_rows[:], ident[:])
-        nc.scalar.activation(out=b_plus[:], in_=b_ps[:, 0:4], func=ACT.Identity, bias=warm_out[:])
 
         dn_wp = keep.tile([P, 2 * R], U8, name="dn_wp", tag="dealt_then_cast", align_bytes=64)
         dn_sp = keep.tile([P, R], U8, name="dn_sp", align_bytes=64)
-        v_first = keep.tile([P, P], U32, name="v_first", align_bytes=64)
-        v_w = keep.tile([P, J], U32, name="v_w", tag="dealt_then_gathered", align_bytes=64)
+        v_w = [
+            keep.tile([P, HALF], U32, name="v_w0", align_bytes=64),
+            keep.tile([P, HALF], U32, name="v_w1", tag="scales_then_words", align_bytes=64),
+        ]
         v_s = keep.tile([P, J], U8, name="v_s", align_bytes=64)
         up_b = [
             keep.tile([P, P * PACK], BF16, name="up_b0", tag="cast_then_h_scales", align_bytes=64),
             keep.tile([P, P * PACK], BF16, name="up_b0b", align_bytes=64),
-            keep.tile([P, N * PACK // 2], BF16, name="up_b1", tag="dealt_then_cast", align_bytes=64),
+            keep.tile([P, P * PACK], BF16, name="up_b2", tag="dealt_then_cast", align_bytes=64),
+            keep.tile([P, P * PACK], BF16, name="up_b3", align_bytes=64),
+        ]
+        up_s = keep.tile([P, N], U8, name="up_s", align_bytes=64)
+        h_b = [
+            keep.tile([P, HALF * PACK], BF16, name="h_b0", align_bytes=64),
+            keep.tile([P, HALF * PACK], BF16, name="h_b1", tag="h_then_codes", align_bytes=64),
         ]
         up_w = [
             keep.tile([P, N // 2], U32, name="up_w0", align_bytes=64),
-            keep.tile([P, N // 2], U32, name="up_w1", tag="x0_0", align_bytes=64),
+            keep.tile([P, N // 2], U32, name="up_w1", tag="h_then_codes", align_bytes=64),
         ]
-        up_s = keep.tile([P, N], U8, name="up_s", align_bytes=64)
-        h_b = keep.tile([P, J * PACK], BF16, name="h_b", align_bytes=64)
+        picked = keep.tile([P, J], F32, name="picked", align_bytes=64)
         h_w = keep.tile([P, J], U32, name="h_w", align_bytes=64)
-        h_s = keep.tile([P, J], U8, name="h_s", tag="cast_then_h_scales", align_bytes=64)
+        h_s0 = keep.tile([P, HALF], U8, name="h_s0", tag="cast_then_h_scales", align_bytes=64)
+        h_s = [h_s0[:], wb8_s[:].bitcast(U8)[4:P, HALF:J]]
         h_ps = [psum.tile([P, PACK, P], F32, name="h_ps%d" % c) for c in range(4)]
         y_ps = [psum.tile([P, J], F32, name="y_ps%d" % i, tag="y_ps%d" % i) for i in range(4)]
-        y_sb = [keep.tile([P, J], F32, name="y_sb%d" % i) for i in range(4)]
+        y_sb = {i: keep.tile([P, J], F32, name="y_sb%d" % i) for i in range(1, 4)}
         res = [keep.tile([P, J], F32, name="res%d" % i) for i in range(4)]
 
         def listed(lo, hi):
@@ -123,8 +125,11 @@ def tile_list_xcross_res_relu_kernel(
         def gather_s(lo, hi):
             nc.vector.tensor_copy(out=v_s[:, lo:hi], in_=tab_s[:].bitcast(U8).indirect(listed(lo, hi)))
 
+        def words(lo, hi):
+            return v_w[lo // HALF][:, lo % HALF : lo % HALF + hi - lo]
+
         def gather_w(lo, hi):
-            nc.vector.tensor_copy(out=v_w[:, lo:hi], in_=tab_w[:].bitcast(U32).indirect(listed(lo, hi)))
+            nc.vector.tensor_copy(out=words(lo, hi), in_=tab_w[:].bitcast(U32).indirect(listed(lo, hi)))
 
         def perm_w():
             nc.vector.tensor_copy(
@@ -145,7 +150,7 @@ def tile_list_xcross_res_relu_kernel(
                     out=h_ps[c][:, t, :],
                     lhsT=dn_wp[:, 2 * t * P : 2 * (t + 1) * P].bitcast(FP4X4),
                     lhsT_scale=dn_sp[:, t * P : (t + 1) * P],
-                    rhs=(v_first[:] if c == 0 else v_w[:, cols]).bitcast(FP8X4),
+                    rhs=words(c * P, (c + 1) * P).bitcast(FP8X4),
                     rhs_scale=v_s[:, cols],
                     start=True,
                     stop=True,
@@ -153,24 +158,15 @@ def tile_list_xcross_res_relu_kernel(
 
         def h_relu(c):
             nc.scalar.activation(
-                out=h_b[:, c * P * PACK : (c + 1) * P * PACK].rearrange("p (j t) -> p j t", t=PACK),
+                out=h_b[c // 2][:, c % 2 * P * PACK : (c % 2 + 1) * P * PACK].rearrange("p (j t) -> p j t", t=PACK),
                 in_=h_ps[c][:].rearrange("p t j -> p j t"),
                 func=ACT.Relu,
             )
 
-        def h_relu_v(c):
-            nc.vector.tensor_scalar(
-                out=h_b[:, c * P * PACK : (c + 1) * P * PACK].rearrange("p (j t) -> p j t", t=PACK),
-                in0=h_ps[c][:].rearrange("p t j -> p j t"),
-                scalar1=0.0,
-                scalar2=None,
-                op0=ALU.max,
-            )
+        def h_quant(half):
+            nc.vector.quantize_mx(out=h_w[:, half * HALF : (half + 1) * HALF].bitcast(FP8X4), scales=h_s[half], in_=h_b[half][:])
 
-        def h_quant(lo, hi):
-            nc.vector.quantize_mx(out=h_w[:, lo:hi].bitcast(FP8X4), scales=h_s[:, lo:hi], in_=h_b[:, lo * PACK : hi * PACK])
-
-        up_cols = ((0, P), (P, 2 * P), (2 * P, N))
+        up_cols = ((0, P), (P, 2 * P), (2 * P, 3 * P), (3 * P, N))
 
         def up_cast(u, on_vector):
             lo, hi = up_cols[u]
@@ -188,44 +184,46 @@ def tile_list_xcross_res_relu_kernel(
                 out=up_w[lo // 256][:, lo - base : hi - base].bitcast(FP8X4), scales=up_s[:, lo:hi], in_=up_b[u][:]
             )
 
-        def pre_gather(i):
-            nc.vector.tensor_copy(out=y_sb[i][:], in_=x0[i][:].indirect(offsets[:]))
+        def pre_gather():
+            nc.vector.tensor_copy(out=picked[:], in_=x0[0][:].indirect(offsets[:]))
 
-        def cross_psum(i):
+        def cross_psum():
             nc.vector.scalar_tensor_tensor(
-                out=res[i][:], in0=y_ps[i][:], scalar=b_plus[:, i : i + 1], in1=y_sb[i][:], op0=ALU.add, op1=ALU.mult
+                out=res[0][:], in0=y_ps[0][:], scalar=b_plus[:, 0:1], in1=picked[:], op0=ALU.add, op1=ALU.mult
             )
 
-        def y_wb4(i, start, stop):
+        def y_wb4(i, c, start):
             nc.tensor.matmul_mx(
-                out=y_ps[i][:],
+                out=y_ps[i][:, c * P : (c + 1) * P],
                 lhsT=wb4_w[:].bitcast(U8)[:, 2 * i * P : 2 * (i + 1) * P].bitcast(FP4X4),
                 lhsT_scale=wb4_s[:].bitcast(U8)[:, i * P : (i + 1) * P],
-                rhs=v_w[:].bitcast(FP8X4),
-                rhs_scale=v_s[:],
+                rhs=words(c * P, (c + 1) * P).bitcast(FP8X4),
+                rhs_scale=v_s[:, c * P : (c + 1) * P],
                 start=start,
-                stop=stop,
+                stop=False,
             )
 
-        def y_wb8(i, start, stop):
+        def y_wb8(i, half, start):
+            cols = slice(half * HALF, (half + 1) * HALF)
             nc.tensor.matmul_mx(
-                out=y_ps[i][:],
+                out=y_ps[i][:, cols],
                 lhsT=wb8_w[:, i * P : (i + 1) * P].bitcast(FP8X4),
                 lhsT_scale=wb8_s[:].bitcast(U8)[:, i * P : (i + 1) * P],
-                rhs=v_w[:].bitcast(FP8X4),
-                rhs_scale=v_s[:],
+                rhs=v_w[half][:].bitcast(FP8X4),
+                rhs_scale=v_s[:, cols],
                 start=start,
-                stop=stop,
+                stop=False,
             )
 
-        def y_up(i, start, stop):
+        def y_up(i, half, stop):
+            cols = slice(half * HALF, (half + 1) * HALF)
             nc.tensor.matmul_mx(
-                out=y_ps[i][:],
+                out=y_ps[i][:, cols],
                 lhsT=up_w[i // 2][:, i % 2 * P : (i % 2 + 1) * P].bitcast(FP8X4),
                 lhsT_scale=up_s[:, i * P : (i + 1) * P],
-                rhs=h_w[:].bitcast(FP8X4),
-                rhs_scale=h_s[:],
-                start=start,
+                rhs=h_w[:, cols].bitcast(FP8X4),
+                rhs_scale=h_s[half],
+                start=False,
                 stop=stop,
             )
 
@@ -239,38 +237,48 @@ def tile_list_xcross_res_relu_kernel(
             nc.sync.dma_start(out=out[i * P : (i + 1) * P, lo:hi], in_=res[i][:, lo:hi])
 
         perm_w()
-        gather_s(0, 512)
-        nc.vector.tensor_copy(out=v_first[:], in_=tab_w[:].bitcast(U32).indirect(listed(0, P)))
         perm_s()
+        gather_w(0, 256)
+        gather_s(0, 128)
         h_mm(0)
-        gather_w(128, 256)
+        gather_s(128, 256)
         h_mm(1)
-        gather_w(256, 512)
+        gather_s(256, 512)
+        gather_w(256, 384)
         h_mm(2)
+        gather_w(384, 512)
         h_mm(3)
-        gather_w(0, 128)
         for c in range(4):
             h_relu(c)
+        nc.scalar.activation(out=b_plus[:], in_=b_ps[:, 0:4], func=ACT.Identity, bias=warm_out[:])
         up_cast(0, True)
         up_cast(1, True)
         up_quant(0)
         up_quant(1)
-        h_quant(0, 256)
-        h_quant(256, 384)
-        h_quant(384, 512)
+        h_quant(0)
+        pre_gather()
+        h_quant(1)
         up_cast(2, False)
-        pre_gather(0)
+        up_cast(3, False)
         up_quant(2)
-        for i in range(4):
-            y_wb8(i, True, False)
+        up_quant(3)
         for i in (1, 0):
-            y_up(i, False, False)
+            for c in range(4):
+                y_wb4(i, c, c == 0)
+            y_up(i, 0, False)
         for i in (1, 0):
-            y_wb4(i, False, True)
+            y_wb8(i, 0, False)
+            y_wb8(i, 1, False)
+        for i in (1, 0):
+            y_up(i, 1, True)
         for i in (2, 3):
-            y_wb4(i, False, False)
-            y_up(i, False, True)
-        cross_psum(0)
+            for half in range(2):
+                y_wb8(i, half, half == 0)
+            for c in range(4):
+                y_wb4(i, c, False)
+            for half in range(2):
+                y_up(i, half, half == 1)
+        cross_psum()
         store(0, 0, J)
         for i in (1, 2):
             y_out(i, 0, J)

@@ -33,9 +33,9 @@ def tile_list_xcross_res_relu_kernel(
 
         offsets = keep.tile([P, J // LIST_ROWS], U16, name="offsets")
         tab_w = keep.tile([P, T], I32, name="tab_w", align_bytes=64)
-        tab_s = keep.tile([P, T // 4], I32, name="tab_s", tag="scales_then_words", align_bytes=64)
+        tab_s = keep.tile([P, T // 4], I32, name="tab_s", align_bytes=64)
         dn_w = keep.tile([P, R // 2], I32, name="dn_w", align_bytes=64)
-        dn_s = keep.tile([P, R // 4], I32, name="dn_s", align_bytes=64)
+        dn_s = keep.tile([P, R // 4], I32, name="dn_s", tag="dealt_then_gathered", align_bytes=64)
         wb4_w = keep.tile([P, N // 2], I32, name="wb4_w", align_bytes=64)
         wb4_s = keep.tile([P, N // 4], I32, name="wb4_s", align_bytes=64)
         wb8_w = keep.tile([P, N], I32, name="wb8_w", align_bytes=64)
@@ -48,10 +48,6 @@ def tile_list_xcross_res_relu_kernel(
         b_plus = keep.tile([P, 4], F32, name="b_plus")
         up_view = upw.rearrange("(p i) n -> p i n", i=PACK)
 
-        def fill_quadrant(queue, plane, src, q):
-            rows = src[0].bitcast(I32)[4 * q : 4 * q + 4, :]
-            queue.dma_start(out=plane[32 * q : 32 * q + 32, :], in_=rows.partition_broadcast(8))
-
         def load_quadrant(queue, plane, src, q):
             queue.dma_start(out=plane[q : P : 32, :], in_=src[0].bitcast(I32)[q : 16 : 4, :])
 
@@ -59,19 +55,20 @@ def tile_list_xcross_res_relu_kernel(
         warm_out = keep.tile([P, 1], F32, name="warm_out")
         nc.vector.memset(tab_s[:], 0)
         nc.vector.memset(warm_in[:], 0.0)
+        nc.vector.memset(dn_s[:], 0)
         nc.gpsimd.memset(b_rows[:], 0.0)
-        nc.sync.dma_start(offsets[:], offs)
-        fill_quadrant(nc.scalar, dn_s, dn_scales, 0)
-        nc.sync.dma_start(out=dn_w[:], in_=dn_words[0].bitcast(I32))
-        fill_quadrant(nc.scalar, dn_s, dn_scales, 1)
-        fill_quadrant(nc.sync, dn_s, dn_scales, 3)
-        fill_quadrant(nc.scalar, dn_s, dn_scales, 2)
-        nc.sync.dma_start(out=tab_w[:], in_=tab_words[0].rearrange("p t i -> p (t i)").bitcast(I32))
-        load_quadrant(nc.scalar, tab_s, tab_scales, 0)
         nc.scalar.activation(out=warm_out[:], in_=warm_in[:], func=ACT.Copy, bias=1.0)
+        nc.sync.dma_start(offsets[:], offs)
+        nc.sync.dma_start(out=dn_w[:], in_=dn_words[0].bitcast(I32))
+        load_quadrant(nc.sync, tab_s, tab_scales, 0)
         load_quadrant(nc.sync, tab_s, tab_scales, 1)
         load_quadrant(nc.sync, tab_s, tab_scales, 2)
         load_quadrant(nc.sync, tab_s, tab_scales, 3)
+        nc.sync.dma_start(out=tab_w[:], in_=tab_words[0].rearrange("p t i -> p (t i)").bitcast(I32))
+        load_quadrant(nc.sync, dn_s, dn_scales, 0)
+        load_quadrant(nc.sync, dn_s, dn_scales, 1)
+        load_quadrant(nc.sync, dn_s, dn_scales, 2)
+        load_quadrant(nc.sync, dn_s, dn_scales, 3)
         nc.sync.dma_start(out=up_raw[0][:], in_=up_view[:, :, 0 : N // 2])
         nc.sync.dma_start(out=wb8_w[:], in_=wb8_words[0].rearrange("p n i -> p (n i)").bitcast(I32))
         for q in range(4):
@@ -87,13 +84,12 @@ def tile_list_xcross_res_relu_kernel(
         nc.gpsimd.dma_start(out=b_rows[0:4, :], in_=b.rearrange("(i p) -> i p", p=P))
         make_identity(nc, ident[:])
         nc.tensor.transpose(b_ps[:], b_rows[:], ident[:])
+        nc.scalar.activation(out=b_plus[:], in_=b_ps[:, 0:4], func=ACT.Identity, bias=warm_out[:])
 
         dn_wp = keep.tile([P, 2 * R], U8, name="dn_wp", tag="dealt_then_cast", align_bytes=64)
         dn_sp = keep.tile([P, R], U8, name="dn_sp", align_bytes=64)
-        v_w = [
-            keep.tile([P, HALF], U32, name="v_w0", align_bytes=64),
-            keep.tile([P, HALF], U32, name="v_w1", tag="scales_then_words", align_bytes=64),
-        ]
+        v_first = keep.tile([P, P], U32, name="v_first", align_bytes=64)
+        v_w = keep.tile([P, J], U32, name="v_w", tag="dealt_then_gathered", align_bytes=64)
         v_s = keep.tile([P, J], U8, name="v_s", align_bytes=64)
         up_b = [
             keep.tile([P, P * PACK], BF16, name="up_b0", tag="cast_then_h_scales", align_bytes=64),
@@ -125,11 +121,8 @@ def tile_list_xcross_res_relu_kernel(
         def gather_s(lo, hi):
             nc.vector.tensor_copy(out=v_s[:, lo:hi], in_=tab_s[:].bitcast(U8).indirect(listed(lo, hi)))
 
-        def words(lo, hi):
-            return v_w[lo // HALF][:, lo % HALF : lo % HALF + hi - lo]
-
         def gather_w(lo, hi):
-            nc.vector.tensor_copy(out=words(lo, hi), in_=tab_w[:].bitcast(U32).indirect(listed(lo, hi)))
+            nc.vector.tensor_copy(out=v_w[:, lo:hi], in_=tab_w[:].bitcast(U32).indirect(listed(lo, hi)))
 
         def perm_w():
             nc.vector.tensor_copy(
@@ -150,7 +143,7 @@ def tile_list_xcross_res_relu_kernel(
                     out=h_ps[c][:, t, :],
                     lhsT=dn_wp[:, 2 * t * P : 2 * (t + 1) * P].bitcast(FP4X4),
                     lhsT_scale=dn_sp[:, t * P : (t + 1) * P],
-                    rhs=words(c * P, (c + 1) * P).bitcast(FP8X4),
+                    rhs=(v_first[:] if c == 0 else v_w[:, cols]).bitcast(FP8X4),
                     rhs_scale=v_s[:, cols],
                     start=True,
                     stop=True,
@@ -192,25 +185,24 @@ def tile_list_xcross_res_relu_kernel(
                 out=res[0][:], in0=y_ps[0][:], scalar=b_plus[:, 0:1], in1=picked[:], op0=ALU.add, op1=ALU.mult
             )
 
-        def y_wb4(i, c, start):
+        def y_wb4(i, start):
             nc.tensor.matmul_mx(
-                out=y_ps[i][:, c * P : (c + 1) * P],
+                out=y_ps[i][:],
                 lhsT=wb4_w[:].bitcast(U8)[:, 2 * i * P : 2 * (i + 1) * P].bitcast(FP4X4),
                 lhsT_scale=wb4_s[:].bitcast(U8)[:, i * P : (i + 1) * P],
-                rhs=words(c * P, (c + 1) * P).bitcast(FP8X4),
-                rhs_scale=v_s[:, c * P : (c + 1) * P],
+                rhs=v_w[:].bitcast(FP8X4),
+                rhs_scale=v_s[:],
                 start=start,
                 stop=False,
             )
 
-        def y_wb8(i, half, start):
-            cols = slice(half * HALF, (half + 1) * HALF)
+        def y_wb8(i, start):
             nc.tensor.matmul_mx(
-                out=y_ps[i][:, cols],
+                out=y_ps[i][:],
                 lhsT=wb8_w[:, i * P : (i + 1) * P].bitcast(FP8X4),
                 lhsT_scale=wb8_s[:].bitcast(U8)[:, i * P : (i + 1) * P],
-                rhs=v_w[half][:].bitcast(FP8X4),
-                rhs_scale=v_s[:, cols],
+                rhs=v_w[:].bitcast(FP8X4),
+                rhs_scale=v_s[:],
                 start=start,
                 stop=False,
             )
@@ -237,20 +229,18 @@ def tile_list_xcross_res_relu_kernel(
             nc.sync.dma_start(out=out[i * P : (i + 1) * P, lo:hi], in_=res[i][:, lo:hi])
 
         perm_w()
+        gather_s(0, 512)
+        nc.vector.tensor_copy(out=v_first[:], in_=tab_w[:].bitcast(U32).indirect(listed(0, P)))
         perm_s()
-        gather_w(0, 256)
-        gather_s(0, 128)
         h_mm(0)
-        gather_s(128, 256)
+        gather_w(128, 256)
         h_mm(1)
-        gather_s(256, 512)
-        gather_w(256, 384)
+        gather_w(256, 512)
         h_mm(2)
-        gather_w(384, 512)
         h_mm(3)
+        gather_w(0, 128)
         for c in range(4):
             h_relu(c)
-        nc.scalar.activation(out=b_plus[:], in_=b_ps[:, 0:4], func=ACT.Identity, bias=warm_out[:])
         up_cast(0, True)
         up_cast(1, True)
         up_quant(0)
@@ -263,19 +253,15 @@ def tile_list_xcross_res_relu_kernel(
         up_quant(2)
         up_quant(3)
         for i in (1, 0):
-            for c in range(4):
-                y_wb4(i, c, c == 0)
+            y_wb4(i, True)
             y_up(i, 0, False)
         for i in (1, 0):
-            y_wb8(i, 0, False)
-            y_wb8(i, 1, False)
+            y_wb8(i, False)
         for i in (1, 0):
             y_up(i, 1, True)
         for i in (2, 3):
-            for half in range(2):
-                y_wb8(i, half, half == 0)
-            for c in range(4):
-                y_wb4(i, c, False)
+            y_wb8(i, True)
+            y_wb4(i, False)
             for half in range(2):
                 y_up(i, half, half == 1)
         cross_psum()

@@ -40,7 +40,7 @@ def tile_list_xcross_res_relu_kernel(
         wb4_s = keep.tile([P, N // 4], I32, name="wb4_s", align_bytes=64)
         wb8_w = keep.tile([P, N], I32, name="wb8_w", align_bytes=64)
         wb8_s = keep.tile([P, N // 4], I32, name="wb8_s", align_bytes=64)
-        up_raw = [keep.tile([P, PACK, N // 2], F32, name="up_raw%d" % u) for u in range(2)]
+        up_raw = [keep.tile([P, PACK, N // 2], F32, name="up_raw%d" % u, tag="up_raw%d" % u, align_bytes=64) for u in range(2)]
         x0 = [keep.tile([P, T], F32, name="x0_%d" % i, tag="x0_%d" % i, align_bytes=64) for i in range(4)]
         b_rows = keep.tile([P, P], F32, name="b_rows")
         ident = keep.tile([P, P], F32, name="ident")
@@ -70,23 +70,27 @@ def tile_list_xcross_res_relu_kernel(
         load_quadrant(nc.sync, dn_s, dn_scales, 2)
         load_quadrant(nc.sync, dn_s, dn_scales, 3)
         nc.sync.dma_start(out=up_raw[0][:], in_=up_view[:, :, 0 : N // 2])
+        for q in (0, 1):
+            load_quadrant(nc.sync, wb8_s, wb8_scales, q)
+        nc.sync.dma_start(out=up_raw[1][:], in_=up_view[:, :, N // 2 : N])
+        for q in (2, 3):
+            load_quadrant(nc.sync, wb8_s, wb8_scales, q)
         nc.sync.dma_start(out=wb8_w[:], in_=wb8_words[0].rearrange("p n i -> p (n i)").bitcast(I32))
-        for q in range(4):
+        nc.sync.dma_start(out=wb4_w[:], in_=wb4_words[0].bitcast(I32))
+        for q in (0, 1):
             load_quadrant(nc.sync, wb4_s, wb4_scales, q)
         nc.sync.dma_start(out=x0[0][:], in_=x0T[0 * P : 1 * P, :])
-        nc.sync.dma_start(out=wb4_w[:], in_=wb4_words[0].bitcast(I32))
-        nc.sync.dma_start(out=up_raw[1][:], in_=up_view[:, :, N // 2 : N])
-        for q in range(4):
-            load_quadrant(nc.sync, wb8_s, wb8_scales, q)
         nc.sync.dma_start(out=x0[1][:], in_=x0T[1 * P : 2 * P, :])
         nc.sync.dma_start(out=x0[2][:], in_=x0T[2 * P : 3 * P, :])
         nc.sync.dma_start(out=x0[3][:], in_=x0T[3 * P : 4 * P, :])
         nc.gpsimd.dma_start(out=b_rows[0:4, :], in_=b.rearrange("(i p) -> i p", p=P))
         make_identity(nc, ident[:])
+        for q in (2, 3):
+            load_quadrant(nc.gpsimd, wb4_s, wb4_scales, q)
         nc.tensor.transpose(b_ps[:], b_rows[:], ident[:])
         nc.scalar.activation(out=b_plus[:], in_=b_ps[:, 0:4], func=ACT.Identity, bias=warm_out[:])
 
-        dn_wp = keep.tile([P, 2 * R], U8, name="dn_wp", tag="dealt_then_cast", align_bytes=64)
+        dn_wp = keep.tile([P, 2 * R], U8, name="dn_wp", align_bytes=64)
         dn_sp = keep.tile([P, R], U8, name="dn_sp", align_bytes=64)
         v_first = keep.tile([P, P], U32, name="v_first", align_bytes=64)
         v_w = keep.tile([P, J], U32, name="v_w", tag="dealt_then_gathered", align_bytes=64)
@@ -94,8 +98,7 @@ def tile_list_xcross_res_relu_kernel(
         up_b = [
             keep.tile([P, P * PACK], BF16, name="up_b0", tag="cast_then_h_scales", align_bytes=64),
             keep.tile([P, P * PACK], BF16, name="up_b0b", align_bytes=64),
-            keep.tile([P, P * PACK], BF16, name="up_b2", tag="dealt_then_cast", align_bytes=64),
-            keep.tile([P, P * PACK], BF16, name="up_b3", align_bytes=64),
+            keep.tile([P, 2 * P * PACK], BF16, name="up_b2", align_bytes=64),
         ]
         up_s = keep.tile([P, N], U8, name="up_s", align_bytes=64)
         h_b = [
@@ -106,13 +109,15 @@ def tile_list_xcross_res_relu_kernel(
             keep.tile([P, N // 2], U32, name="up_w0", align_bytes=64),
             keep.tile([P, N // 2], U32, name="up_w1", tag="h_then_codes", align_bytes=64),
         ]
-        picked = keep.tile([P, J], F32, name="picked", align_bytes=64)
         h_w = keep.tile([P, J], U32, name="h_w", align_bytes=64)
-        h_s0 = keep.tile([P, HALF], U8, name="h_s0", tag="cast_then_h_scales", align_bytes=64)
-        h_s = [h_s0[:], wb8_s[:].bitcast(U8)[4:P, HALF:J]]
-        h_ps = [psum.tile([P, PACK, P], F32, name="h_ps%d" % c) for c in range(4)]
+        h_s = [
+            keep.tile([P, HALF], U8, name="h_s0", tag="cast_then_h_scales", align_bytes=64),
+            keep.tile([P, HALF], U8, name="h_s1", tag="up_raw1", align_bytes=64),
+        ]
+        h_ps = [psum.tile([P, PACK, P], F32, name="h_ps%d" % c, tag="h_ps%d" % c) for c in range(4)]
         y_ps = [psum.tile([P, J], F32, name="y_ps%d" % i, tag="y_ps%d" % i) for i in range(4)]
-        y_sb = {i: keep.tile([P, J], F32, name="y_sb%d" % i) for i in range(1, 4)}
+        y_late = psum.tile([P, J], F32, name="y_late", tag="h_ps0")
+        y_sb = [keep.tile([P, J], F32, name="y_sb%d" % i) for i in range(4)]
         res = [keep.tile([P, J], F32, name="res%d" % i) for i in range(4)]
 
         def listed(lo, hi):
@@ -157,9 +162,9 @@ def tile_list_xcross_res_relu_kernel(
             )
 
         def h_quant(half):
-            nc.vector.quantize_mx(out=h_w[:, half * HALF : (half + 1) * HALF].bitcast(FP8X4), scales=h_s[half], in_=h_b[half][:])
+            nc.vector.quantize_mx(out=h_w[:, half * HALF : (half + 1) * HALF].bitcast(FP8X4), scales=h_s[half][:], in_=h_b[half][:])
 
-        up_cols = ((0, P), (P, 2 * P), (2 * P, 3 * P), (3 * P, N))
+        up_cols = ((0, P), (P, 2 * P), (2 * P, N))
 
         def up_cast(u, on_vector):
             lo, hi = up_cols[u]
@@ -177,32 +182,27 @@ def tile_list_xcross_res_relu_kernel(
                 out=up_w[lo // 256][:, lo - base : hi - base].bitcast(FP8X4), scales=up_s[:, lo:hi], in_=up_b[u][:]
             )
 
-        def pre_gather():
-            nc.vector.tensor_copy(out=picked[:], in_=x0[0][:].indirect(offsets[:]))
+        def y_sum(i, lo, hi):
+            return (y_late if i == 0 and lo >= HALF else y_ps[i])[:, lo:hi]
 
-        def cross_psum():
-            nc.vector.scalar_tensor_tensor(
-                out=res[0][:], in0=y_ps[0][:], scalar=b_plus[:, 0:1], in1=picked[:], op0=ALU.add, op1=ALU.mult
-            )
-
-        def y_wb4(i, start):
+        def y_wb4(i, lo, hi, start, stop):
             nc.tensor.matmul_mx(
-                out=y_ps[i][:],
+                out=y_sum(i, lo, hi),
                 lhsT=wb4_w[:].bitcast(U8)[:, 2 * i * P : 2 * (i + 1) * P].bitcast(FP4X4),
                 lhsT_scale=wb4_s[:].bitcast(U8)[:, i * P : (i + 1) * P],
-                rhs=v_w[:].bitcast(FP8X4),
-                rhs_scale=v_s[:],
+                rhs=v_w[:, lo:hi].bitcast(FP8X4),
+                rhs_scale=v_s[:, lo:hi],
                 start=start,
-                stop=False,
+                stop=stop,
             )
 
-        def y_wb8(i, start):
+        def y_wb8(i, lo, hi, start):
             nc.tensor.matmul_mx(
-                out=y_ps[i][:],
+                out=y_sum(i, lo, hi),
                 lhsT=wb8_w[:, i * P : (i + 1) * P].bitcast(FP8X4),
                 lhsT_scale=wb8_s[:].bitcast(U8)[:, i * P : (i + 1) * P],
-                rhs=v_w[:].bitcast(FP8X4),
-                rhs_scale=v_s[:],
+                rhs=v_w[:, lo:hi].bitcast(FP8X4),
+                rhs_scale=v_s[:, lo:hi],
                 start=start,
                 stop=False,
             )
@@ -210,17 +210,17 @@ def tile_list_xcross_res_relu_kernel(
         def y_up(i, half, stop):
             cols = slice(half * HALF, (half + 1) * HALF)
             nc.tensor.matmul_mx(
-                out=y_ps[i][:, cols],
+                out=y_sum(i, half * HALF, (half + 1) * HALF),
                 lhsT=up_w[i // 2][:, i % 2 * P : (i % 2 + 1) * P].bitcast(FP8X4),
                 lhsT_scale=up_s[:, i * P : (i + 1) * P],
                 rhs=h_w[:, cols].bitcast(FP8X4),
-                rhs_scale=h_s[half],
+                rhs_scale=h_s[half][:],
                 start=False,
                 stop=stop,
             )
 
         def y_out(i, lo, hi):
-            nc.scalar.activation(out=y_sb[i][:, lo:hi], in_=y_ps[i][:, lo:hi], func=ACT.Identity, bias=b_plus[:, i : i + 1])
+            nc.scalar.activation(out=y_sb[i][:, lo:hi], in_=y_sum(i, lo, hi), func=ACT.Identity, bias=b_plus[:, i : i + 1])
 
         def cross(i, lo, hi):
             nc.vector.tensor_tensor(out=res[i][:, lo:hi], in0=x0[i][:].indirect(listed(lo, hi)), in1=y_sb[i][:, lo:hi], op=ALU.mult)
@@ -246,25 +246,27 @@ def tile_list_xcross_res_relu_kernel(
         up_quant(0)
         up_quant(1)
         h_quant(0)
-        pre_gather()
+        up_cast(2, True)
         h_quant(1)
-        up_cast(2, False)
-        up_cast(3, False)
         up_quant(2)
-        up_quant(3)
-        for i in (1, 0):
-            y_wb4(i, True)
-            y_up(i, 0, False)
-        for i in (1, 0):
-            y_wb8(i, False)
-        for i in (1, 0):
-            y_up(i, 1, True)
-        for i in (2, 3):
-            y_wb8(i, True)
-            y_wb4(i, False)
+        y_wb8(0, 0, HALF, True)
+        y_up(0, 0, False)
+        y_wb4(0, 0, P, False, False)
+        y_wb4(0, P, HALF, False, True)
+        y_wb4(0, HALF, HALF + P, True, False)
+        y_wb4(0, HALF + P, J, False, False)
+        y_wb8(0, HALF, J, False)
+        y_wb4(1, 0, J, True, False)
+        y_up(0, 1, True)
+        for i in (1, 2, 3):
+            if i > 1:
+                y_wb4(i, 0, J, True, False)
+            y_wb8(i, 0, J, False)
             for half in range(2):
                 y_up(i, half, half == 1)
-        cross_psum()
+        for lo, hi in ((0, HALF), (HALF, J)):
+            y_out(0, lo, hi)
+            cross(0, lo, hi)
         store(0, 0, J)
         for i in (1, 2):
             y_out(i, 0, J)

@@ -70,14 +70,13 @@ def tile_list_xcross_res_relu_kernel(
         load_quadrant(nc.sync, dn_s, dn_scales, 2)
         load_quadrant(nc.sync, dn_s, dn_scales, 3)
         nc.sync.dma_start(out=up_raw[0][:], in_=up_view[:, :, 0 : N // 2])
-        for q in (0, 1):
+        for q in (0, 1, 2):
             load_quadrant(nc.sync, wb8_s, wb8_scales, q)
         nc.sync.dma_start(out=up_raw[1][:], in_=up_view[:, :, N // 2 : N])
-        for q in (2, 3):
-            load_quadrant(nc.sync, wb8_s, wb8_scales, q)
+        load_quadrant(nc.sync, wb8_s, wb8_scales, 3)
         nc.sync.dma_start(out=wb8_w[:], in_=wb8_words[0].rearrange("p n i -> p (n i)").bitcast(I32))
         nc.sync.dma_start(out=wb4_w[:], in_=wb4_words[0].bitcast(I32))
-        for q in (0, 1):
+        for q in (0, 1, 2):
             load_quadrant(nc.sync, wb4_s, wb4_scales, q)
         nc.sync.dma_start(out=x0[0][:], in_=x0T[0 * P : 1 * P, :])
         nc.sync.dma_start(out=x0[1][:], in_=x0T[1 * P : 2 * P, :])
@@ -85,8 +84,7 @@ def tile_list_xcross_res_relu_kernel(
         nc.sync.dma_start(out=x0[3][:], in_=x0T[3 * P : 4 * P, :])
         nc.gpsimd.dma_start(out=b_rows[0:4, :], in_=b.rearrange("(i p) -> i p", p=P))
         make_identity(nc, ident[:])
-        for q in (2, 3):
-            load_quadrant(nc.gpsimd, wb4_s, wb4_scales, q)
+        load_quadrant(nc.gpsimd, wb4_s, wb4_scales, 3)
         nc.tensor.transpose(b_ps[:], b_rows[:], ident[:])
         nc.scalar.activation(out=b_plus[:], in_=b_ps[:, 0:4], func=ACT.Identity, bias=warm_out[:])
 
@@ -257,11 +255,12 @@ def tile_list_xcross_res_relu_kernel(
         y_wb4(0, HALF + P, J, False, False)
         y_wb8(0, HALF, J, False)
         y_wb4(1, 0, J, True, False)
+        y_wb8(1, 0, J, False)
         y_up(0, 1, True)
         for i in (1, 2, 3):
             if i > 1:
                 y_wb4(i, 0, J, True, False)
-            y_wb8(i, 0, J, False)
+                y_wb8(i, 0, J, False)
             for half in range(2):
                 y_up(i, half, half == 1)
         for lo, hi in ((0, HALF), (HALF, J)):

@@ -53,10 +53,12 @@ def tile_list_xcross_res_relu_kernel(
 
         warm_in = keep.tile([P, 1], F32, name="warm_in")
         warm_out = keep.tile([P, 1], F32, name="warm_out")
-        nc.vector.memset(tab_s[:], 0)
+        nc.gpsimd.memset(tab_s[:], 0)
         nc.vector.memset(warm_in[:], 0.0)
         nc.vector.memset(dn_s[:], 0)
-        nc.gpsimd.memset(b_rows[:], 0.0)
+        nc.gpsimd.dma_start(out=b_rows[0:32, :], in_=b.rearrange("(i p) -> i p", p=P).partition_broadcast(8))
+        nc.gpsimd.memset(b_rows[32:64, :], 0.0)
+        nc.gpsimd.memset(b_rows[64:P, :], 0.0)
         nc.scalar.activation(out=warm_out[:], in_=warm_in[:], func=ACT.Copy, bias=1.0)
         nc.sync.dma_start(offsets[:], offs)
         nc.sync.dma_start(out=dn_w[:], in_=dn_words[0].bitcast(I32))
@@ -82,7 +84,6 @@ def tile_list_xcross_res_relu_kernel(
         nc.sync.dma_start(out=x0[1][:], in_=x0T[1 * P : 2 * P, :])
         nc.sync.dma_start(out=x0[2][:], in_=x0T[2 * P : 3 * P, :])
         nc.sync.dma_start(out=x0[3][:], in_=x0T[3 * P : 4 * P, :])
-        nc.gpsimd.dma_start(out=b_rows[0:4, :], in_=b.rearrange("(i p) -> i p", p=P))
         make_identity(nc, ident[:])
         load_quadrant(nc.gpsimd, wb4_s, wb4_scales, 3)
         nc.tensor.transpose(b_ps[:], b_rows[:], ident[:])

@@ -57,8 +57,9 @@ def tile_list_xcross_res_relu_kernel(
         nc.vector.memset(warm_in[:], 0.0)
         nc.vector.memset(dn_s[:], 0)
         nc.gpsimd.dma_start(out=b_rows[0:32, :], in_=b.rearrange("(i p) -> i p", p=P).partition_broadcast(8))
-        nc.gpsimd.memset(b_rows[32:64, :], 0.0)
-        nc.gpsimd.memset(b_rows[64:P, :], 0.0)
+        nc.vector.memset(ident[:], 0.0)
+        nc.vector.memset(b_rows[32:64, :], 0.0)
+        nc.vector.memset(b_rows[64:P, :], 0.0)
         nc.scalar.activation(out=warm_out[:], in_=warm_in[:], func=ACT.Copy, bias=1.0)
         nc.sync.dma_start(offsets[:], offs)
         nc.sync.dma_start(out=dn_w[:], in_=dn_words[0].bitcast(I32))
@@ -84,7 +85,7 @@ def tile_list_xcross_res_relu_kernel(
         nc.sync.dma_start(out=x0[1][:], in_=x0T[1 * P : 2 * P, :])
         nc.sync.dma_start(out=x0[2][:], in_=x0T[2 * P : 3 * P, :])
         nc.sync.dma_start(out=x0[3][:], in_=x0T[3 * P : 4 * P, :])
-        make_identity(nc, ident[:])
+        make_identity(nc, ident[:], nomemset=True)
         load_quadrant(nc.gpsimd, wb4_s, wb4_scales, 3)
         nc.tensor.transpose(b_ps[:], b_rows[:], ident[:])
         nc.scalar.activation(out=b_plus[:], in_=b_ps[:, 0:4], func=ACT.Identity, bias=warm_out[:])

@@ -1,7 +1,6 @@
 from contextlib import ExitStack
 
 import concourse.mybir as mybir
-from concourse.masks import make_identity
 
 K, R, N, T, J = 512, 512, 512, 1024, 512
 FLOPS = 2 * J * (K * R + 2 * K * N + R * N)
@@ -37,97 +36,99 @@ def tile_list_xcross_res_relu_kernel(
         dn_w = keep.tile([P, R // 2], I32, name="dn_w", align_bytes=64)
         dn_s = keep.tile([P, R // 4], I32, name="dn_s", tag="dealt_then_gathered", align_bytes=64)
         wb4_w = keep.tile([P, N // 2], I32, name="wb4_w", align_bytes=64)
-        wb4_s = keep.tile([P, N // 4], I32, name="wb4_s", align_bytes=64)
         wb8_w = keep.tile([P, N], I32, name="wb8_w", align_bytes=64)
-        wb8_s = keep.tile([P, N // 4], I32, name="wb8_s", align_bytes=64)
+        wb_s = keep.tile([P, 2 * N // 4], I32, name="wb_s", align_bytes=64)
         up_raw = [keep.tile([P, PACK, N // 2], F32, name="up_raw%d" % u, tag="up_raw%d" % u, align_bytes=64) for u in range(2)]
         x0 = [keep.tile([P, T], F32, name="x0_%d" % i, tag="x0_%d" % i, align_bytes=64) for i in range(4)]
-        b_rows = keep.tile([P, P], F32, name="b_rows")
-        ident = keep.tile([P, P], F32, name="ident")
-        b_ps = psum.tile([P, P], F32, name="b_ps", tag="y_ps3")
+        b_rows = keep.tile([P, 32], F32, name="b_rows", align_bytes=64)
         b_plus = keep.tile([P, 4], F32, name="b_plus")
         up_view = upw.rearrange("(p i) n -> p i n", i=PACK)
 
         def load_quadrant(queue, plane, src, q):
             queue.dma_start(out=plane[q : P : 32, :], in_=src[0].bitcast(I32)[q : 16 : 4, :])
 
+        def load_spread(plane, src):
+            nc.sync.dma_start(out=plane[0:P:8], in_=src[0].bitcast(I32))
+
         warm_in = keep.tile([P, 1], F32, name="warm_in")
         warm_out = keep.tile([P, 1], F32, name="warm_out")
         nc.gpsimd.memset(tab_s[:], 0)
         nc.vector.memset(warm_in[:], 0.0)
-        nc.vector.memset(dn_s[:], 0)
-        nc.gpsimd.dma_start(out=b_rows[0:32, :], in_=b.rearrange("(i p) -> i p", p=P).partition_broadcast(8))
-        nc.vector.memset(ident[:], 0.0)
-        nc.vector.memset(b_rows[32:64, :], 0.0)
-        nc.vector.memset(b_rows[64:P, :], 0.0)
+        nc.gpsimd.memset(dn_s[:], 0)
+        nc.vector.memset(wb_s[:], 0)
+        nc.vector.memset(b_rows[:], 0.0)
+        load_quadrant(nc.gpsimd, dn_s, dn_scales, 3)
         nc.scalar.activation(out=warm_out[:], in_=warm_in[:], func=ACT.Copy, bias=1.0)
         nc.sync.dma_start(offsets[:], offs)
         nc.sync.dma_start(out=dn_w[:], in_=dn_words[0].bitcast(I32))
-        load_quadrant(nc.sync, tab_s, tab_scales, 0)
-        load_quadrant(nc.sync, tab_s, tab_scales, 1)
-        load_quadrant(nc.sync, tab_s, tab_scales, 2)
-        load_quadrant(nc.sync, tab_s, tab_scales, 3)
+        for q in range(4):
+            load_quadrant(nc.sync, tab_s, tab_scales, q)
         nc.sync.dma_start(out=tab_w[:], in_=tab_words[0].rearrange("p t i -> p (t i)").bitcast(I32))
-        load_quadrant(nc.sync, dn_s, dn_scales, 0)
-        load_quadrant(nc.sync, dn_s, dn_scales, 1)
-        load_quadrant(nc.sync, dn_s, dn_scales, 2)
-        load_quadrant(nc.sync, dn_s, dn_scales, 3)
+        for q in range(3):
+            load_quadrant(nc.sync, dn_s, dn_scales, q)
         nc.sync.dma_start(out=up_raw[0][:], in_=up_view[:, :, 0 : N // 2])
-        for q in (0, 1, 2):
-            load_quadrant(nc.sync, wb8_s, wb8_scales, q)
+        load_spread(wb_s[:, 0 : N // 4], wb8_scales)
+        load_spread(wb_s[:, N // 4 : N // 2], wb4_scales)
         nc.sync.dma_start(out=up_raw[1][:], in_=up_view[:, :, N // 2 : N])
-        load_quadrant(nc.sync, wb8_s, wb8_scales, 3)
+        nc.sync.dma_start(out=b_rows[0:P:8, :], in_=b.rearrange("(i q c) -> q i c", i=4, q=4))
         nc.sync.dma_start(out=wb8_w[:], in_=wb8_words[0].rearrange("p n i -> p (n i)").bitcast(I32))
         nc.sync.dma_start(out=wb4_w[:], in_=wb4_words[0].bitcast(I32))
-        for q in (0, 1, 2):
-            load_quadrant(nc.sync, wb4_s, wb4_scales, q)
-        nc.sync.dma_start(out=x0[0][:], in_=x0T[0 * P : 1 * P, :])
-        nc.sync.dma_start(out=x0[1][:], in_=x0T[1 * P : 2 * P, :])
-        nc.sync.dma_start(out=x0[2][:], in_=x0T[2 * P : 3 * P, :])
-        nc.sync.dma_start(out=x0[3][:], in_=x0T[3 * P : 4 * P, :])
-        make_identity(nc, ident[:], nomemset=True)
-        load_quadrant(nc.gpsimd, wb4_s, wb4_scales, 3)
-        nc.tensor.transpose(b_ps[:], b_rows[:], ident[:])
-        nc.scalar.activation(out=b_plus[:], in_=b_ps[:, 0:4], func=ACT.Identity, bias=warm_out[:])
+        for r in (1, 2, 3):
+            nc.sync.dma_start(out=wb_s[r:P:32, :], in_=wb_s[8 * r : P : 32, :])
+        for i in range(4):
+            nc.sync.dma_start(out=x0[i][:], in_=x0T[i * P : (i + 1) * P, :])
 
         dn_wp = keep.tile([P, 2 * R], U8, name="dn_wp", align_bytes=64)
         dn_sp = keep.tile([P, R], U8, name="dn_sp", align_bytes=64)
-        v_first = keep.tile([P, P], U32, name="v_first", align_bytes=64)
-        v_w = keep.tile([P, J], U32, name="v_w", tag="dealt_then_gathered", align_bytes=64)
+        v_w = [
+            keep.tile([P, HALF], U32, name="v_w0", align_bytes=64),
+            keep.tile([P, HALF], U32, name="v_w1", tag="dealt_then_gathered", align_bytes=64),
+        ]
         v_s = keep.tile([P, J], U8, name="v_s", align_bytes=64)
         up_b = [
-            keep.tile([P, P * PACK], BF16, name="up_b0", tag="cast_then_h_scales", align_bytes=64),
+            keep.tile([P, P * PACK], BF16, name="up_b0", align_bytes=64),
             keep.tile([P, P * PACK], BF16, name="up_b0b", align_bytes=64),
             keep.tile([P, 2 * P * PACK], BF16, name="up_b2", align_bytes=64),
         ]
+        b_cols = keep.tile([P, 32], F32, name="b_cols", tag="up_raw0", align_bytes=64)
         up_s = keep.tile([P, N], U8, name="up_s", align_bytes=64)
         h_b = [
             keep.tile([P, HALF * PACK], BF16, name="h_b0", align_bytes=64),
-            keep.tile([P, HALF * PACK], BF16, name="h_b1", tag="h_then_codes", align_bytes=64),
+            keep.tile([P, HALF * PACK], BF16, name="h_b1", align_bytes=64),
         ]
         up_w = [
             keep.tile([P, N // 2], U32, name="up_w0", align_bytes=64),
-            keep.tile([P, N // 2], U32, name="up_w1", tag="h_then_codes", align_bytes=64),
+            keep.tile([P, N // 2], U32, name="up_w1", align_bytes=64),
         ]
         h_w = keep.tile([P, J], U32, name="h_w", align_bytes=64)
-        h_s = [
-            keep.tile([P, HALF], U8, name="h_s0", tag="cast_then_h_scales", align_bytes=64),
-            keep.tile([P, HALF], U8, name="h_s1", tag="up_raw1", align_bytes=64),
-        ]
+        h_s = keep.tile([P, J], U8, name="h_s", tag="up_raw1", align_bytes=64)
         h_ps = [psum.tile([P, PACK, P], F32, name="h_ps%d" % c, tag="h_ps%d" % c) for c in range(4)]
-        y_ps = [psum.tile([P, J], F32, name="y_ps%d" % i, tag="y_ps%d" % i) for i in range(4)]
-        y_late = psum.tile([P, J], F32, name="y_late", tag="h_ps0")
+        banks = {
+            (0, 0): "y_a",
+            (0, HALF): "y_c",
+            (0, HALF + P): "h_ps0",
+            (1, 0): "y_b",
+            (1, HALF): "h_ps1",
+            (2, 0): "h_ps2",
+            (2, HALF): "h_ps3",
+            (3, 0): "y_a",
+            (3, HALF): "y_c",
+        }
+        y_ps = {key: psum.tile([P, J], F32, name="y_ps%d_%d" % key, tag=tag) for key, tag in banks.items()}
         y_sb = [keep.tile([P, J], F32, name="y_sb%d" % i) for i in range(4)]
         res = [keep.tile([P, J], F32, name="res%d" % i) for i in range(4)]
 
         def listed(lo, hi):
             return offsets[:, lo // LIST_ROWS : hi // LIST_ROWS]
 
-        def gather_s(lo, hi):
-            nc.vector.tensor_copy(out=v_s[:, lo:hi], in_=tab_s[:].bitcast(U8).indirect(listed(lo, hi)))
+        def cols_of(half):
+            return slice(half * HALF, (half + 1) * HALF)
 
-        def gather_w(lo, hi):
-            nc.vector.tensor_copy(out=v_w[:, lo:hi], in_=tab_w[:].bitcast(U32).indirect(listed(lo, hi)))
+        def gather_s():
+            nc.vector.tensor_copy(out=v_s[:], in_=tab_s[:].bitcast(U8).indirect(listed(0, J)))
+
+        def gather_w(half):
+            nc.vector.tensor_copy(out=v_w[half][:], in_=tab_w[:].bitcast(U32).indirect(listed(half * HALF, (half + 1) * HALF)))
 
         def perm_w():
             nc.vector.tensor_copy(
@@ -136,20 +137,20 @@ def tile_list_xcross_res_relu_kernel(
             )
 
         def perm_s():
-            nc.vector.tensor_copy(
-                out=dn_sp[:].rearrange("p (t m) -> p t m", t=PACK),
-                in_=dn_s[:].bitcast(U8).rearrange("p (m t) -> p t m", t=PACK),
-            )
+            for t in (0, 2):
+                nc.vector.tensor_copy(
+                    out=dn_sp[:].rearrange("p (t m) -> p t m", t=PACK)[:, t : t + 2, :],
+                    in_=dn_s[:].bitcast(U8).rearrange("p (m t) -> p t m", t=PACK)[:, t : t + 2, :],
+                )
 
         def h_mm(c):
-            cols = slice(c * P, (c + 1) * P)
             for t in range(PACK):
                 nc.tensor.matmul_mx(
                     out=h_ps[c][:, t, :],
                     lhsT=dn_wp[:, 2 * t * P : 2 * (t + 1) * P].bitcast(FP4X4),
                     lhsT_scale=dn_sp[:, t * P : (t + 1) * P],
-                    rhs=(v_first[:] if c == 0 else v_w[:, cols]).bitcast(FP8X4),
-                    rhs_scale=v_s[:, cols],
+                    rhs=v_w[c // 2][:, c % 2 * P : (c % 2 + 1) * P].bitcast(FP8X4),
+                    rhs_scale=v_s[:, c * P : (c + 1) * P],
                     start=True,
                     stop=True,
                 )
@@ -161,19 +162,22 @@ def tile_list_xcross_res_relu_kernel(
                 func=ACT.Relu,
             )
 
-        def h_quant(half):
-            nc.vector.quantize_mx(out=h_w[:, half * HALF : (half + 1) * HALF].bitcast(FP8X4), scales=h_s[half][:], in_=h_b[half][:])
+        def h_quant(lo, hi):
+            half, base = lo // HALF, lo // HALF * HALF
+            nc.vector.quantize_mx(
+                out=h_w[:, lo:hi].bitcast(FP8X4),
+                scales=h_s[:, lo:hi],
+                in_=h_b[half][:, (lo - base) * PACK : (hi - base) * PACK],
+            )
 
         up_cols = ((0, P), (P, 2 * P), (2 * P, N))
 
-        def up_cast(u, on_vector):
+        def up_cast(u):
             lo, hi = up_cols[u]
-            dst = up_b[u][:].rearrange("p (c e i) -> p c i e", e=4, i=PACK)
-            src = up_raw[lo // 256][:, :, lo % 256 : lo % 256 + hi - lo].rearrange("p i (c e) -> p c i e", e=4)
-            if on_vector:
-                nc.vector.tensor_copy(out=dst, in_=src)
-            else:
-                nc.scalar.copy(out=dst, in_=src)
+            nc.vector.tensor_copy(
+                out=up_b[u][:].rearrange("p (c e i) -> p c i e", e=4, i=PACK),
+                in_=up_raw[lo // 256][:, :, lo % 256 : lo % 256 + hi - lo].rearrange("p i (c e) -> p c i e", e=4),
+            )
 
         def up_quant(u):
             lo, hi = up_cols[u]
@@ -183,39 +187,42 @@ def tile_list_xcross_res_relu_kernel(
             )
 
         def y_sum(i, lo, hi):
-            return (y_late if i == 0 and lo >= HALF else y_ps[i])[:, lo:hi]
+            return y_ps[i, lo][:, lo:hi]
 
-        def y_wb4(i, lo, hi, start, stop):
+        def words(lo, hi):
+            base = lo // HALF * HALF
+            return v_w[lo // HALF][:, lo - base : hi - base].bitcast(FP8X4)
+
+        def y_wb4(i, lo, hi, stop=False):
             nc.tensor.matmul_mx(
                 out=y_sum(i, lo, hi),
                 lhsT=wb4_w[:].bitcast(U8)[:, 2 * i * P : 2 * (i + 1) * P].bitcast(FP4X4),
-                lhsT_scale=wb4_s[:].bitcast(U8)[:, i * P : (i + 1) * P],
-                rhs=v_w[:, lo:hi].bitcast(FP8X4),
+                lhsT_scale=wb_s[:].bitcast(U8)[:, N + i * P : N + (i + 1) * P],
+                rhs=words(lo, hi),
                 rhs_scale=v_s[:, lo:hi],
-                start=start,
+                start=False,
                 stop=stop,
             )
 
-        def y_wb8(i, lo, hi, start):
+        def y_wb8(i, lo, hi, start=False):
             nc.tensor.matmul_mx(
                 out=y_sum(i, lo, hi),
                 lhsT=wb8_w[:, i * P : (i + 1) * P].bitcast(FP8X4),
-                lhsT_scale=wb8_s[:].bitcast(U8)[:, i * P : (i + 1) * P],
-                rhs=v_w[:, lo:hi].bitcast(FP8X4),
+                lhsT_scale=wb_s[:].bitcast(U8)[:, i * P : (i + 1) * P],
+                rhs=words(lo, hi),
                 rhs_scale=v_s[:, lo:hi],
                 start=start,
                 stop=False,
             )
 
-        def y_up(i, half, stop):
-            cols = slice(half * HALF, (half + 1) * HALF)
+        def y_up(i, lo, hi, start=False, stop=False):
             nc.tensor.matmul_mx(
-                out=y_sum(i, half * HALF, (half + 1) * HALF),
+                out=y_sum(i, lo, hi),
                 lhsT=up_w[i // 2][:, i % 2 * P : (i % 2 + 1) * P].bitcast(FP8X4),
                 lhsT_scale=up_s[:, i * P : (i + 1) * P],
-                rhs=h_w[:, cols].bitcast(FP8X4),
-                rhs_scale=h_s[half][:],
-                start=False,
+                rhs=h_w[:, lo:hi].bitcast(FP8X4),
+                rhs_scale=h_s[:, lo:hi],
+                start=start,
                 stop=stop,
             )
 
@@ -229,51 +236,62 @@ def tile_list_xcross_res_relu_kernel(
             nc.sync.dma_start(out=out[i * P : (i + 1) * P, lo:hi], in_=res[i][:, lo:hi])
 
         perm_w()
-        gather_s(0, 512)
-        nc.vector.tensor_copy(out=v_first[:], in_=tab_w[:].bitcast(U32).indirect(listed(0, P)))
+        gather_s()
+        gather_w(0)
         perm_s()
         h_mm(0)
-        gather_w(128, 256)
         h_mm(1)
-        gather_w(256, 512)
+        gather_w(1)
         h_mm(2)
         h_mm(3)
-        gather_w(0, 128)
         for c in range(4):
             h_relu(c)
-        up_cast(0, True)
-        up_cast(1, True)
+        up_cast(0)
+        up_cast(1)
         up_quant(0)
         up_quant(1)
-        h_quant(0)
-        up_cast(2, True)
-        h_quant(1)
+        halves = ((0, HALF), (HALF, J))
+        third, fourth = (HALF, HALF + P), (HALF + P, J)
+        up_cast(2)
+        nc.vector.transpose(b_cols[:], b_rows[:])
+        h_quant(0, HALF)
+        nc.vector.tensor_scalar(out=b_plus[:], in0=b_cols[:, 0:32:8], scalar1=warm_out[:], scalar2=None, op0=ALU.add)
         up_quant(2)
-        y_wb8(0, 0, HALF, True)
-        y_up(0, 0, False)
-        y_wb4(0, 0, P, False, False)
-        y_wb4(0, P, HALF, False, True)
-        y_wb4(0, HALF, HALF + P, True, False)
-        y_wb4(0, HALF + P, J, False, False)
-        y_wb8(0, HALF, J, False)
-        y_wb4(1, 0, J, True, False)
-        y_wb8(1, 0, J, False)
-        y_up(0, 1, True)
-        for i in (1, 2, 3):
-            if i > 1:
-                y_wb4(i, 0, J, True, False)
-                y_wb8(i, 0, J, False)
-            for half in range(2):
-                y_up(i, half, half == 1)
-        for lo, hi in ((0, HALF), (HALF, J)):
-            y_out(0, lo, hi)
-            cross(0, lo, hi)
+        h_quant(*third)
+        h_quant(*fourth)
+        for lo, hi in (halves[0], third):
+            y_wb8(0, lo, hi, start=True)
+            y_wb4(0, lo, hi)
+            y_up(0, lo, hi, stop=True)
+        y_wb8(0, *fourth, start=True)
+        y_wb4(0, *fourth)
+        y_wb8(1, 0, HALF, start=True)
+        y_wb4(1, 0, HALF)
+        y_up(0, *fourth, stop=True)
+        y_up(1, 0, HALF, stop=True)
+        y_wb8(1, HALF, J, start=True)
+        y_wb4(1, HALF, J)
+        y_up(1, HALF, J, stop=True)
+        y_out(0, 0, HALF)
+        cross(0, 0, HALF)
+        y_out(0, *third)
+        y_out(0, *fourth)
+        cross(0, HALF, J)
         store(0, 0, J)
-        for i in (1, 2):
-            y_out(i, 0, J)
-            cross(i, 0, J)
-            store(i, 0, J)
-        y_out(3, 0, J)
-        for lo, hi in ((0, 256), (256, 512)):
+        for lo, hi in halves:
+            y_out(1, lo, hi)
+            cross(1, lo, hi)
+        store(1, 0, J)
+        for i in (2, 3):
+            for lo, hi in halves:
+                y_wb8(i, lo, hi, start=True)
+                y_wb4(i, lo, hi)
+                y_up(i, lo, hi, stop=True)
+        for lo, hi in halves:
+            y_out(2, lo, hi)
+        cross(2, 0, J)
+        store(2, 0, J)
+        for lo, hi in halves:
+            y_out(3, lo, hi)
             cross(3, lo, hi)
             store(3, lo, hi)

@@ -44,8 +44,8 @@ def tile_list_xcross_res_relu_kernel(
         b_plus = keep.tile([P, 4], F32, name="b_plus")
         up_view = upw.rearrange("(p i) n -> p i n", i=PACK)
 
-        def load_quadrant(queue, plane, src, q):
-            queue.dma_start(out=plane[q : P : 32, :], in_=src[0].bitcast(I32)[q : 16 : 4, :])
+        def load_quadrant(plane, src, q):
+            nc.sync.dma_start(out=plane[q : P : 32, :], in_=src[0].bitcast(I32)[q : 16 : 4, :])
 
         def load_spread(plane, src):
             nc.sync.dma_start(out=plane[0:P:8], in_=src[0].bitcast(I32))
@@ -57,15 +57,14 @@ def tile_list_xcross_res_relu_kernel(
         nc.gpsimd.memset(dn_s[:], 0)
         nc.vector.memset(wb_s[:], 0)
         nc.vector.memset(b_rows[:], 0.0)
-        load_quadrant(nc.gpsimd, dn_s, dn_scales, 3)
         nc.scalar.activation(out=warm_out[:], in_=warm_in[:], func=ACT.Copy, bias=1.0)
         nc.sync.dma_start(offsets[:], offs)
         nc.sync.dma_start(out=dn_w[:], in_=dn_words[0].bitcast(I32))
         for q in range(4):
-            load_quadrant(nc.sync, tab_s, tab_scales, q)
+            load_quadrant(tab_s, tab_scales, q)
         nc.sync.dma_start(out=tab_w[:], in_=tab_words[0].rearrange("p t i -> p (t i)").bitcast(I32))
-        for q in range(3):
-            load_quadrant(nc.sync, dn_s, dn_scales, q)
+        for q in range(4):
+            load_quadrant(dn_s, dn_scales, q)
         nc.sync.dma_start(out=up_raw[0][:], in_=up_view[:, :, 0 : N // 2])
         load_spread(wb_s[:, 0 : N // 4], wb8_scales)
         load_spread(wb_s[:, N // 4 : N // 2], wb4_scales)

from contextlib import ExitStack

import concourse.mybir as mybir

K, R, N, T, J = 512, 512, 512, 1024, 512
FLOPS = 2 * J * (K * R + 2 * K * N + R * N)

F32 = mybir.dt.float32
BF16 = mybir.dt.bfloat16
I32 = mybir.dt.int32
U32 = mybir.dt.uint32
U16 = mybir.dt.uint16
U8 = mybir.dt.uint8
FP8X4 = mybir.dt.float8_e4m3fn_x4
FP4X4 = mybir.dt.float4_e2m1fn_x4
ACT = mybir.ActivationFunctionType
ALU = mybir.AluOpType

P = 128
PACK = 4
LIST_ROWS = 16
HALF = J // 2


def tile_list_xcross_res_relu_kernel(
    tc, tab_words, tab_scales, wb4_words, wb4_scales, wb8_words, wb8_scales, dn_words, dn_scales, upw, x0T, b, offs, out
):
    nc = tc.nc
    with ExitStack() as ctx:
        keep = ctx.enter_context(tc.tile_pool(name="keep", bufs=1))
        psum = ctx.enter_context(tc.psum_pool(name="psum", bufs=1))

        offsets = keep.tile([P, J // LIST_ROWS], U16, name="offsets")
        tab_w = keep.tile([P, T], I32, name="tab_w", align_bytes=64)
        tab_s = keep.tile([P, T // 4], I32, name="tab_s", align_bytes=64)
        dn_w = keep.tile([P, R // 2], I32, name="dn_w", align_bytes=64)
        dn_s = keep.tile([P, R // 4], I32, name="dn_s", tag="dealt_then_gathered", align_bytes=64)
        wb4_w = keep.tile([P, N // 2], I32, name="wb4_w", align_bytes=64)
        wb8_w = keep.tile([P, N], I32, name="wb8_w", align_bytes=64)
        wb_s = keep.tile([P, 2 * N // 4], I32, name="wb_s", align_bytes=64)
        up_raw = [keep.tile([P, PACK, N // 2], F32, name="up_raw%d" % u, tag="up_raw%d" % u, align_bytes=64) for u in range(2)]
        x0 = [keep.tile([P, T], F32, name="x0_%d" % i, tag="x0_%d" % i, align_bytes=64) for i in range(4)]
        b_rows = keep.tile([P, 32], F32, name="b_rows", align_bytes=64)
        b_plus = keep.tile([P, 4], F32, name="b_plus")
        up_view = upw.rearrange("(p i) n -> p i n", i=PACK)

        def load_quadrant(plane, src, q):
            nc.sync.dma_start(out=plane[q : P : 32, :], in_=src[0].bitcast(I32)[q : 16 : 4, :])

        def load_spread(plane, src):
            nc.sync.dma_start(out=plane[0:P:8], in_=src[0].bitcast(I32))

        warm_in = keep.tile([P, 1], F32, name="warm_in")
        warm_out = keep.tile([P, 1], F32, name="warm_out")
        nc.gpsimd.memset(tab_s[:], 0)
        nc.vector.memset(warm_in[:], 0.0)
        nc.gpsimd.memset(dn_s[:], 0)
        nc.vector.memset(wb_s[:], 0)
        nc.vector.memset(b_rows[:], 0.0)
        nc.scalar.activation(out=warm_out[:], in_=warm_in[:], func=ACT.Copy, bias=1.0)
        nc.sync.dma_start(offsets[:], offs)
        nc.sync.dma_start(out=dn_w[:], in_=dn_words[0].bitcast(I32))
        for q in range(4):
            load_quadrant(tab_s, tab_scales, q)
        nc.sync.dma_start(out=tab_w[:], in_=tab_words[0].rearrange("p t i -> p (t i)").bitcast(I32))
        for q in range(4):
            load_quadrant(dn_s, dn_scales, q)
        nc.sync.dma_start(out=up_raw[0][:], in_=up_view[:, :, 0 : N // 2])
        load_spread(wb_s[:, 0 : N // 4], wb8_scales)
        load_spread(wb_s[:, N // 4 : N // 2], wb4_scales)
        nc.sync.dma_start(out=up_raw[1][:], in_=up_view[:, :, N // 2 : N])
        nc.sync.dma_start(out=b_rows[0:P:8, :], in_=b.rearrange("(i q c) -> q i c", i=4, q=4))
        nc.sync.dma_start(out=wb8_w[:], in_=wb8_words[0].rearrange("p n i -> p (n i)").bitcast(I32))
        nc.sync.dma_start(out=wb4_w[:], in_=wb4_words[0].bitcast(I32))
        for r in (1, 2, 3):
            nc.sync.dma_start(out=wb_s[r:P:32, :], in_=wb_s[8 * r : P : 32, :])
        for i in range(4):
            nc.sync.dma_start(out=x0[i][:], in_=x0T[i * P : (i + 1) * P, :])

        dn_wp = keep.tile([P, 2 * R], U8, name="dn_wp", align_bytes=64)
        dn_sp = keep.tile([P, R], U8, name="dn_sp", align_bytes=64)
        v_w = [
            keep.tile([P, HALF], U32, name="v_w0", align_bytes=64),
            keep.tile([P, HALF], U32, name="v_w1", tag="dealt_then_gathered", align_bytes=64),
        ]
        v_s = keep.tile([P, J], U8, name="v_s", align_bytes=64)
        up_b = [
            keep.tile([P, P * PACK], BF16, name="up_b0", align_bytes=64),
            keep.tile([P, P * PACK], BF16, name="up_b0b", align_bytes=64),
            keep.tile([P, 2 * P * PACK], BF16, name="up_b2", align_bytes=64),
        ]
        b_cols = keep.tile([P, 32], F32, name="b_cols", tag="up_raw0", align_bytes=64)
        up_s = keep.tile([P, N], U8, name="up_s", align_bytes=64)
        h_b = [
            keep.tile([P, HALF * PACK], BF16, name="h_b0", align_bytes=64),
            keep.tile([P, HALF * PACK], BF16, name="h_b1", align_bytes=64),
        ]
        up_w = [
            keep.tile([P, N // 2], U32, name="up_w0", align_bytes=64),
            keep.tile([P, N // 2], U32, name="up_w1", align_bytes=64),
        ]
        h_w = keep.tile([P, J], U32, name="h_w", align_bytes=64)
        h_s = keep.tile([P, J], U8, name="h_s", tag="up_raw1", align_bytes=64)
        h_ps = [psum.tile([P, PACK, P], F32, name="h_ps%d" % c, tag="h_ps%d" % c) for c in range(4)]
        banks = {
            (0, 0): "y_a",
            (0, HALF): "y_c",
            (0, HALF + P): "h_ps0",
            (1, 0): "y_b",
            (1, HALF): "h_ps1",
            (2, 0): "h_ps2",
            (2, HALF): "h_ps3",
            (3, 0): "y_a",
            (3, HALF): "y_c",
        }
        y_ps = {key: psum.tile([P, J], F32, name="y_ps%d_%d" % key, tag=tag) for key, tag in banks.items()}
        y_sb = [keep.tile([P, J], F32, name="y_sb%d" % i) for i in range(4)]
        res = [keep.tile([P, J], F32, name="res%d" % i) for i in range(4)]

        def listed(lo, hi):
            return offsets[:, lo // LIST_ROWS : hi // LIST_ROWS]

        def cols_of(half):
            return slice(half * HALF, (half + 1) * HALF)

        def gather_s():
            nc.vector.tensor_copy(out=v_s[:], in_=tab_s[:].bitcast(U8).indirect(listed(0, J)))

        def gather_w(half):
            nc.vector.tensor_copy(out=v_w[half][:], in_=tab_w[:].bitcast(U32).indirect(listed(half * HALF, (half + 1) * HALF)))

        def perm_w():
            nc.vector.tensor_copy(
                out=dn_wp[:].bitcast(U16).rearrange("p (t m) -> p t m", t=PACK),
                in_=dn_w[:].bitcast(U16).rearrange("p (m t) -> p t m", t=PACK),
            )

        def perm_s():
            for t in (0, 2):
                nc.vector.tensor_copy(
                    out=dn_sp[:].rearrange("p (t m) -> p t m", t=PACK)[:, t : t + 2, :],
                    in_=dn_s[:].bitcast(U8).rearrange("p (m t) -> p t m", t=PACK)[:, t : t + 2, :],
                )

        def h_mm(c):
            for t in range(PACK):
                nc.tensor.matmul_mx(
                    out=h_ps[c][:, t, :],
                    lhsT=dn_wp[:, 2 * t * P : 2 * (t + 1) * P].bitcast(FP4X4),
                    lhsT_scale=dn_sp[:, t * P : (t + 1) * P],
                    rhs=v_w[c // 2][:, c % 2 * P : (c % 2 + 1) * P].bitcast(FP8X4),
                    rhs_scale=v_s[:, c * P : (c + 1) * P],
                    start=True,
                    stop=True,
                )

        def h_relu(c):
            nc.scalar.activation(
                out=h_b[c // 2][:, c % 2 * P * PACK : (c % 2 + 1) * P * PACK].rearrange("p (j t) -> p j t", t=PACK),
                in_=h_ps[c][:].rearrange("p t j -> p j t"),
                func=ACT.Relu,
            )

        def h_quant(lo, hi):
            half, base = lo // HALF, lo // HALF * HALF
            nc.vector.quantize_mx(
                out=h_w[:, lo:hi].bitcast(FP8X4),
                scales=h_s[:, lo:hi],
                in_=h_b[half][:, (lo - base) * PACK : (hi - base) * PACK],
            )

        up_cols = ((0, P), (P, 2 * P), (2 * P, N))

        def up_cast(u):
            lo, hi = up_cols[u]
            nc.vector.tensor_copy(
                out=up_b[u][:].rearrange("p (c e i) -> p c i e", e=4, i=PACK),
                in_=up_raw[lo // 256][:, :, lo % 256 : lo % 256 + hi - lo].rearrange("p i (c e) -> p c i e", e=4),
            )

        def up_quant(u):
            lo, hi = up_cols[u]
            base = lo // 256 * 256
            nc.vector.quantize_mx(
                out=up_w[lo // 256][:, lo - base : hi - base].bitcast(FP8X4), scales=up_s[:, lo:hi], in_=up_b[u][:]
            )

        def y_sum(i, lo, hi):
            return y_ps[i, lo][:, lo:hi]

        def words(lo, hi):
            base = lo // HALF * HALF
            return v_w[lo // HALF][:, lo - base : hi - base].bitcast(FP8X4)

        def y_wb4(i, lo, hi, stop=False):
            nc.tensor.matmul_mx(
                out=y_sum(i, lo, hi),
                lhsT=wb4_w[:].bitcast(U8)[:, 2 * i * P : 2 * (i + 1) * P].bitcast(FP4X4),
                lhsT_scale=wb_s[:].bitcast(U8)[:, N + i * P : N + (i + 1) * P],
                rhs=words(lo, hi),
                rhs_scale=v_s[:, lo:hi],
                start=False,
                stop=stop,
            )

        def y_wb8(i, lo, hi, start=False):
            nc.tensor.matmul_mx(
                out=y_sum(i, lo, hi),
                lhsT=wb8_w[:, i * P : (i + 1) * P].bitcast(FP8X4),
                lhsT_scale=wb_s[:].bitcast(U8)[:, i * P : (i + 1) * P],
                rhs=words(lo, hi),
                rhs_scale=v_s[:, lo:hi],
                start=start,
                stop=False,
            )

        def y_up(i, lo, hi, start=False, stop=False):
            nc.tensor.matmul_mx(
                out=y_sum(i, lo, hi),
                lhsT=up_w[i // 2][:, i % 2 * P : (i % 2 + 1) * P].bitcast(FP8X4),
                lhsT_scale=up_s[:, i * P : (i + 1) * P],
                rhs=h_w[:, lo:hi].bitcast(FP8X4),
                rhs_scale=h_s[:, lo:hi],
                start=start,
                stop=stop,
            )

        def y_out(i, lo, hi):
            nc.scalar.activation(out=y_sb[i][:, lo:hi], in_=y_sum(i, lo, hi), func=ACT.Identity, bias=b_plus[:, i : i + 1])

        def cross(i, lo, hi):
            nc.vector.tensor_tensor(out=res[i][:, lo:hi], in0=x0[i][:].indirect(listed(lo, hi)), in1=y_sb[i][:, lo:hi], op=ALU.mult)

        def store(i, lo, hi):
            nc.sync.dma_start(out=out[i * P : (i + 1) * P, lo:hi], in_=res[i][:, lo:hi])

        perm_w()
        gather_s()
        gather_w(0)
        perm_s()
        h_mm(0)
        h_mm(1)
        gather_w(1)
        h_mm(2)
        h_mm(3)
        for c in range(4):
            h_relu(c)
        up_cast(0)
        up_cast(1)
        up_quant(0)
        up_quant(1)
        halves = ((0, HALF), (HALF, J))
        third, fourth = (HALF, HALF + P), (HALF + P, J)
        up_cast(2)
        nc.vector.transpose(b_cols[:], b_rows[:])
        h_quant(0, HALF)
        nc.vector.tensor_scalar(out=b_plus[:], in0=b_cols[:, 0:32:8], scalar1=warm_out[:], scalar2=None, op0=ALU.add)
        up_quant(2)
        h_quant(*third)
        h_quant(*fourth)
        for lo, hi in (halves[0], third):
            y_wb8(0, lo, hi, start=True)
            y_wb4(0, lo, hi)
            y_up(0, lo, hi, stop=True)
        y_wb8(0, *fourth, start=True)
        y_wb4(0, *fourth)
        y_wb8(1, 0, HALF, start=True)
        y_wb4(1, 0, HALF)
        y_up(0, *fourth, stop=True)
        y_up(1, 0, HALF, stop=True)
        y_wb8(1, HALF, J, start=True)
        y_wb4(1, HALF, J)
        y_up(1, HALF, J, stop=True)
        y_out(0, 0, HALF)
        cross(0, 0, HALF)
        y_out(0, *third)
        y_out(0, *fourth)
        cross(0, HALF, J)
        store(0, 0, J)
        for lo, hi in halves:
            y_out(1, lo, hi)
            cross(1, lo, hi)
        store(1, 0, J)
        for i in (2, 3):
            for lo, hi in halves:
                y_wb8(i, lo, hi, start=True)
                y_wb4(i, lo, hi)
                y_up(i, lo, hi, stop=True)
        for lo, hi in halves:
            y_out(2, lo, hi)
        cross(2, 0, J)
        store(2, 0, J)
        for lo, hi in halves:
            y_out(3, lo, hi)
            cross(3, lo, hi)
            store(3, lo, hi)
